import numpy as np, ml_dtypes
CORES = [9,25,41,57]
N = 4
BF = ml_dtypes.bfloat16
def f(rng, *shape):
    return (rng.standard_normal(shape, dtype=np.float32) * np.exp2(rng.integers(-2, 3, shape[:-1] + (1,)))).astype(BF)
def wide(rng, *shape):
    v = f(rng, *shape).astype(np.float32); k = shape[:-2] + (1, shape[-1])
    return (v * np.exp2(rng.integers(-6, 7, k)) * (rng.random(k) > 0.0625)).astype(BF)
def entries(a):
    return np.ascontiguousarray(a.T).reshape(-1)
def table(e):
    return np.ascontiguousarray(np.reshape(e, (-1, 16)).T).astype(np.int32)
def gentries(a):
    return np.ascontiguousarray(a.reshape(8, 16, -1).transpose(0, 2, 1)).reshape(8, -1)
def gtable(e):
    e = np.asarray(e); return np.ascontiguousarray(e.reshape(8, -1, 16).transpose(0, 2, 1)).reshape(128, -1).astype(np.int32)
C, S, STEPS, X, NB = 2048, 64, 6, 4, 128
def others(r):
    a = np.arange(N * S); return a[a // S != r]
def field(v):
    return np.clip(v.astype(np.float32), -16, 16).astype(BF)
def draw(rng, every=False):
    s = rng.integers(0, C, (N, 8, C)); sd = np.zeros((N, N, S), np.int64); inner = []
    for r in range(N):
        p = rng.permutation(C); nb = NB
        if every:
            nb = N * S; p = p[(p > 0) & (p < C - 1)]; e = p[:nb - 2]; p = np.concatenate([[0, C - 1], p])
            sd[r] = np.roll(np.concatenate([[0], e[:2 * S - 2], [C - 1], e[2 * S - 2:]]).reshape(N, S), r + 1, axis=0)
        else:
            sd[r] = np.stack([rng.permutation(p[:nb])[:S] for q in range(N)])
        inner.append(p[nb:])
        s[r][rng.random((8, C)) < 0.125] = -1
        o = others(r)
        for g in range(8): s[r, g, rng.permutation(p[nb:])[:len(o)]] = C + rng.permutation(o)
    return s, sd, inner
def pack(rng, s, sd):
    m = [(rng.standard_normal((128, 128)) * 128 ** -0.5 * z).clip(-1, 1).astype(BF) for z in (0.85, 1.0)]
    return {"flow": field(f(rng, N, 128, C).astype(np.float32) * np.float32(0.5)), "mix": np.stack([m[0]] * N), "bend": np.stack([m[1]] * N),
            "links": np.stack([gtable(s[r]) for r in range(N)]), "sends": np.stack([table(sd[r].reshape(-1)) for r in range(N)])}
def setup_inputs(rng):
    s, sd, inner = draw(rng); return pack(rng, s, sd)
def setup_inputs_walls(rng):
    s, sd, inner = draw(rng, True)
    for r in range(N):
        o = rng.permutation(8); s[r][:, rng.permutation(C)[:256]] = -1; s[r][:, [0, C - 1]] = -1
        s[r, o[0]] = -1; s[r, o[1]] = np.where(s[r, o[1]] < 0, np.arange(C), s[r, o[1]])
    return pack(rng, s, sd)
def setup_inputs_repeats(rng):
    s, sd, inner = draw(rng)
    for r in range(N):
        o = rng.permutation(8); c = rng.integers(0, C, 8); c[o[0]] = 0; c[o[1]] = C - 1; e = others(r)
        near = (s[r] >= 0) & (s[r] < C) & (rng.random((8, C)) < 0.75)
        s[r] = np.where(near, c[:, None], s[r])
        s[r, o[2]] = np.where(s[r, o[2]] >= C, C + e[-1], s[r, o[2]]); s[r, o[3]] = np.where(s[r, o[3]] >= C, C + e[0], s[r, o[3]])
        sd[r, (r + 1) % N] = sd[r, (r + 1) % N, 0]
    return pack(rng, s, sd)
def setup_inputs_far(rng):
    s, sd, inner = draw(rng)
    for r in range(N):
        e = others(r); k = inner[r]; s[r][:, k] = C + rng.choice(e, (8, len(k)))
        s[r][:, k[0]] = C + e[0]; s[r][:, k[1]] = C + e[-1]
    return pack(rng, s, sd)
def setup_inputs_spread(rng):
    d = setup_inputs(rng); d["flow"] = field(wide(rng, N, 128, C).astype(np.float32) * np.float32(2.0 ** -7)); return d
def check_inputs(d):
    bad = []
    for a, b in (("flow", 16), ("mix", 1), ("bend", 1)):
        x = d[a].astype(np.float64)
        if not (np.abs(x) <= b).all(): bad.append(a + ": size")
        if a != "flow" and not (x == x[:1]).all(): bad.append(a + ": not alike on all ranks")
    s = np.stack([gentries(d["links"][r]) for r in range(N)]).astype(np.int64); sd = np.stack([entries(d["sends"][r]) for r in range(N)]).astype(np.int64)
    if (s < -1).any() or (s >= C + N * S).any(): bad.append("links: range")
    if (sd < 0).any() or (sd >= C).any(): bad.append("sends: range")
    if bad: return bad
    for r in range(N):
        if ((s[r] >= C) & ((s[r] - C) // S == r)).any(): bad.append("links: own rank's arrivals")
        if (s[r][:, sd[r]] >= C).any(): bad.append("a cell that is sent takes from another rank")
    if not bad:
        with np.errstate(all="ignore"): v, top = run(**d)
        if not (top <= 1024): bad.append("h or v of a step: size")
    return bad
def run(flow, mix, bend, links, sends):
    v = flow.astype(np.float64); m = mix.astype(np.float64); b = bend.astype(np.float64); top = 0.0
    s = np.stack([gentries(links[r]) for r in range(N)]).astype(np.int64)[:, :, None, :]
    sd = np.stack([entries(sends[r]).reshape(N, S) for r in range(N)]).astype(np.int64)
    opp = np.arange(8) ^ X
    for t in range(STEPS):
        h = np.stack([m[r].T @ v[r] + 0.125 * (b[r].T @ v[r]) ** 2 for r in range(N)])
        top = np.maximum(top, np.max(np.abs(h)))
        new = []
        for r in range(N):
            w = np.concatenate([h[r]] + [h[q][:, sd[q, r]] for q in range(N)], axis=1).reshape(8, 16, C + N * S)
            got = np.take_along_axis(w, np.maximum(s[r], 0), axis=2)
            new.append(np.where(s[r] < 0, h[r].reshape(8, 16, C)[opp], got).reshape(128, C))
        v = np.stack(new)
    return v, top
def reference(flow, mix, bend, links, sends):
    v, top = run(flow, mix, bend, links, sends)
    return {"y": v.astype(np.float32)}

@@ -1,0 +1,327 @@
+from concourse.bass import DstId, RemoteDMATransfer
+from concourse.mybir import AluOpType as Alu, ActivationFunctionType as Act
+
+C, S, STEPS, N = 2048, 64, 6, 4
+NS = (N - 1) * S
+H0 = NS
+A0 = H0 + C
+O0 = A0 + N * S
+WL = O0 + C
+
+CHUNKS = [("0", 512, "f", 1), ("1", 288, "x", 2), ("2", 512, "f", 3), ("3", 384, "x", 0), ("4", 224, "f", 1), ("5", 128, "f", 2)]
+ORDER = {
+    "A": ["G0", "QS", "G2", "H3", "Q0", "Q1", "M3", "Q2", "G4", "G5", "Q3", "Q4", "Q5"],
+    "D": ["GS0", "GS1", "H1", "DS", "R1", "M1", "L1", "R3", "D0", "D1", "L3", "D2", "D3", "D4", "D5"],
+    "P": ["BS0", "AS0", "BS1", "AS1", "h1", "B0", "A0", "m1", "B1", "A1", "h3", "B2", "A2", "m3", "B3", "A3", "B4", "A4", "B5", "A5"],
+}
+SWAPS = [["0"], ["S"], ["1"], ["2"], ["3"], ["4", "5"]]
+LAST = {
+    "A": [("F", 128, 256), ("F", 512, 800), ("F", 1056, 1312), ("X", 0, 0), ("X", 1, 0), ("F", 1888, 2048)],
+    "D": [("F", 0, 128), ("F", 256, 512), ("F", 800, 1056), ("F", 1312, 1696), ("F", 1696, 1888)],
+}
+STORES = [(0, 256), (256, 800), (800, 1312), (1312, 1696), (1696, 2048)]
+
+SCRATCH = {
+    "fl": ("sbuf", [128, C], "bfloat16"), "fs": ("sbuf", [128, NS], "bfloat16"),
+    "mixb": ("sbuf", [128, 128], "bfloat16"), "bendb": ("sbuf", [128, 128], "bfloat16"),
+    "mixf": ("sbuf", [128, 128], "float32"), "bendf": ("sbuf", [128, 128], "float32"),
+    "hs": ("sbuf", [128, STEPS * NS], "float32"),
+    "v": ("sbuf", [128, C], "float32"), "vs": ("sbuf", [128, NS], "float32"), "res": ("sbuf", [128, C], "float32"),
+    "hi": ("sbuf", [128, C], "bfloat16"), "mid": ("sbuf", [128, C], "bfloat16"), "lo": ("sbuf", [128, C], "bfloat16"),
+    "sq": ("sbuf", [128, C], "float32"), "sqs": ("sbuf", [128, NS], "float32"),
+    "lk": ("sbuf", [128, 128], "int32"), "si": ("sbuf", [128, 36], "int32"), "sf": ("sbuf", [128, 36], "float32"),
+    "su": ("sbuf", [128, 36], "uint16"), "off": ("sbuf", [128, 128], "uint16"), "offs": ("sbuf", [128, 12], "uint16"),
+    "di": ("sbuf", [128, NS], "int32"), "dj": ("sbuf", [128, NS], "int32"), "diag": ("sbuf", [128, NS], "float32"),
+    "pm": ("sbuf", [128, 4], "float32"), "k0": ("sbuf", [128, 128], "float32"), "kn": ("sbuf", [128, 128], "float32"),
+    "k2": ("sbuf", [128, 12], "float32"), "ones": ("sbuf", [128, 128], "float32"), "bd0": ("sbuf", [128, 128], "float32"),
+    "bd": ("sbuf", [128, 128], "float32"), "nf": ("sbuf", [128, NS], "float32"), "mk": ("sbuf", [128, NS], "float32"),
+    "xx": ("sbuf", [128, NS], "float32"), "yy": ("sbuf", [128, NS], "float32"), "zz": ("sbuf", [128, NS], "float32"),
+    "t1": ("sbuf", [128, 128], "float32"), "t2": ("sbuf", [128, 128], "float32"),
+    "t3": ("sbuf", [128, 12], "float32"), "t4": ("sbuf", [128, 12], "float32"),
+}
+for _t in range(STEPS):
+    SCRATCH["w%d" % _t] = ("sbuf", [128, WL], "float32")
+for _b in range(8):
+    SCRATCH["ps%d" % _b] = ("psum", [128, 512], "float32")
+
+SEMAPHORES = (["cA", "cD", "cP", "cG", "lds", "ldf", "ldl", "ldw", "sent", "stored"]
+              + ["arr%d" % t for t in range(STEPS)]
+              + ["op%d_%d" % (t, k) for t in range(STEPS) for k in range(8)])
+
+
+def rank_program(g, core, T, topo):
+    rank = T.rank_of(core)
+    if rank is None:
+        return
+    queue = {"A": g.scalar, "D": g.vector, "P": g.tensor, "G": g, "S": g.sync}
+    calls = {q: [] for q in queue}
+    outside = {}
+
+    def put(q, name, emit, deps=(), sem=None, inc=1):
+        calls[q].append((name, emit, list(deps), sem or "c" + q, inc))
+
+    def dma(q, name, pairs, deps, sem):
+        put(q, name, [(lambda o=o, i=i: queue[q].dma_start(o, i)) for o, i in pairs], deps, sem, 16)
+
+    W = [T["w%d" % t] for t in range(STEPS)]
+    ps = [T["ps%d" % b] for b in range(8)]
+    V, A, P = g.vector, g.scalar, g.tensor
+    others = [r for r in range(N) if r != rank]
+    root8 = 0.125 ** 0.5
+
+    pieces = []
+    if rank > 0:
+        pieces.append((T.si[0:16, 0:4 * rank], T.sends[:, 0:4 * rank]))
+    if rank < N - 1:
+        pieces.append((T.si[0:16, 4 * rank:12], T.sends[:, 4 * rank + 4:16]))
+    dma("A", "ld_s", pieces, [], "lds")
+    dma("A", "ld_l", [(T.lk[:], T.links[:])], [], "ldl")
+    dma("S", "ld_f", [(T.fl[:], T.flow[:])], [], "ldf")
+    dma("S", "ld_w", [(T.bendb[:], T.bend[:]), (T.mixb[:], T.mix[:])], [], "ldw")
+
+    put("G", "di", [lambda: g.iota(T.di[:], [[0, 12], [-1, 16]], 16, 1)])
+    put("G", "k0", [lambda: g.iota(T.k0[:], [[-16, 128]], -(O0 - H0), 0, allow_small_or_imprecise_dtypes=True)])
+    put("G", "ones", [lambda: g.iota(T.ones[:], [[0, 128]], 1, 0, allow_small_or_imprecise_dtypes=True)])
+    put("G", "bd0", [lambda: g.affine_select(T.bd0[:], T.ones[:], [[-16, 8], [0, 16]], Alu.is_ge, 0.0, 0, 1)], ["ones"])
+    put("G", "bd", [lambda: g.affine_select(T.bd[:], T.bd0[:], [[16, 8], [0, 16]], Alu.is_ge, 0.0, 15, -1)], ["bd0"])
+    own = A0 + rank * S
+    for t in range(STEPS):
+        put("D", "own%d" % t, [lambda t=t: V.memset(W[t][:, own:own + S], 0.0)])
+    put("D", "nf0", [lambda: V.memset(T.nf[:], 1.0)])
+    put("D", "dj", [lambda: V.tensor_scalar(T.dj[:], T.di[:], 15, None, Alu.bitwise_and)], ["di"])
+    put("D", "nf", [lambda: V.memset(T.nf[:, 0:NS:16], 0.0)], ["nf0"])
+    put("D", "diag", [lambda: V.tensor_scalar(T.diag[:], T.dj[:], 0.0, None, Alu.is_equal)], ["dj"])
+    put("D", "pm", [lambda: V.tensor_copy(T.pm[:, 0:1], T.dj[:, 0:1])], ["dj"])
+    put("D", "kn", [lambda: V.tensor_scalar(T.kn[:], T.k0[:], T.pm[:, 0:1], None, Alu.subtract)], ["pm", "k0"])
+    put("D", "k2", [lambda: V.tensor_scalar(T.k2[:], T.kn[:, 0:12], float(O0), None, Alu.add)], ["kn"])
+
+    put("D", "s_hi", [lambda: V.tensor_scalar(T.si[0:16, 12:24], T.si[0:16, 0:12], 4, None, Alu.arith_shift_right)], ["ld_s"])
+    put("D", "s_lo", [lambda: V.tensor_scalar(T.si[0:16, 24:36], T.si[0:16, 0:12], 15, None, Alu.bitwise_and)], ["ld_s"])
+    put("D", "sf", [lambda: V.tensor_copy(T.sf[0:16, :], T.si[0:16, :])], ["s_hi", "s_lo"])
+    put("P", "rep", [lambda: P.matmul(ps[6][:, 0:36], T.diag[0:16, 0:128], T.sf[0:16, :], True, True)], ["sf", "diag"])
+    put("D", "su", [lambda: V.tensor_copy(T.su[:], ps[6][:, 0:36])], ["rep"])
+    put("D", "mk", [lambda: V.tensor_copy(T.mk[:], T.diag[:, 0:16].indirect(T.su[:, 24:36]))], ["su"])
+    put("D", "t1", [lambda: V.tensor_tensor(T.t1[:], T.lk[:], T.kn[:], Alu.mult)], ["ld_l", "kn"])
+    put("D", "xx", [lambda: V.tensor_tensor(T.xx[:], T.lk[:, 0:128].indirect(T.su[:, 12:24]), T.mk[:], Alu.mult)], ["mk", "ld_l"])
+    put("D", "t2", [lambda: V.tensor_tensor(T.t2[:], T.t1[:], T.lk[:], Alu.max)], ["t1"])
+    put("A", "bendf", [lambda: A.activation(T.bendf[:], T.bendb[:], Act.Copy)], ["ld_w"])
+    put("A", "mixf", [lambda: A.activation(T.mixf[:], T.mixb[:], Act.Copy)], ["ld_w"])
+
+    def send(t):
+        moves = []
+        for d in range(1, N):
+            r = (rank + d) % N
+            dst = T.cores[r]
+            eng = topo.engines(core, dst)
+            pick = [eng[0::2], eng[1::2], eng][d - 1]
+            rid, pid = topo.addr(dst)[0:2]
+            j = t * NS + others.index(r) * S
+            moves.append(RemoteDMATransfer(dst_ids=[DstId(rid=rid, pnc=pid)], dma_engine_mask=sum(1 << e for e in pick),
+                                           remote_sem=T.sem["arr%d" % t], src=T.hs[:, j:j + S], dst=W[t][:, own:own + S]))
+        n = len(topo.engines(core, T.cores[others[0]]))
+        outside["arr%d" % t] = ("arr%d" % t, 2 * n)
+        put("G", "send%d" % t, [lambda: (g.remote_dma_fused(moves[0:2], local_sem=T.sem.sent), None)[1],
+                                lambda: (g.remote_dma_fused(moves[2:3], local_sem=T.sem.sent), None)[1]], ["DS_%d" % t], "sent", n)
+
+    def halves(t, a, b):
+        return [(W[t][0:64, O0 + a:O0 + b], W[t][64:128, H0 + a:H0 + b]), (W[t][64:128, O0 + a:O0 + b], W[t][0:64, H0 + a:H0 + b])]
+
+    def swap(t, k, a, b, deps):
+        dma("S", "op%d_%d" % (k, t), halves(t, a, b), deps, "op%d_%d" % (t, k))
+
+    def swap_sent(t):
+        j = t * NS
+        dma("S", "opS_%d" % t, [(W[t][0:64, 0:NS], T.hs[64:128, j:j + NS]), (W[t][64:128, 0:NS], T.hs[0:64, j:j + NS])],
+            ["DS_%d" % t], "op%d_7" % t)
+
+    def square(name, out, pair, n, deps):
+        put("A", name, [lambda: A.activation(out, ps[2 * pair][:, 0:n], Act.Square, scale=root8)], deps)
+
+    def total(name, out, pair, n, sq, deps):
+        put("D", name, [lambda: V.tensor_tensor(out, ps[2 * pair + 1][:, 0:n], sq, Alu.add)], deps)
+
+    def mm1(name, bank, w, rhs, n, deps):
+        put("P", name, [lambda: P.matmul(ps[bank][:, 0:n], w[:], rhs, True, True)], deps)
+
+    put("A", "GS_0", [lambda: A.activation(T.fs[:], T.fl[:, 0:C].indirect(T.su[:, 0:12]), Act.Copy)], ["su", "ld_f"])
+    first = [(0, 512, 1), (512, 1024, 2), (1024, 1536, 0), (1536, 2048, 1)]
+    mm1("B0_0", 2, T.bendb, T.fl[:, 0:512], 512, ["ld_f", "ld_w"])
+    mm1("BS_0", 0, T.bendb, T.fs[:], NS, ["GS_0"])
+    mm1("AS_0", 1, T.mixb, T.fs[:], NS, [])
+    mm1("A0_0", 3, T.mixb, T.fl[:, 0:512], 512, [])
+    square("QS_0", T.sqs[:], 0, NS, ["BS_0"])
+    total("DS_0", T.hs[:, 0:NS], 0, NS, T.sqs[:], ["AS_0", "QS_0"])
+    send(0)
+    swap_sent(0)
+    put("P", "e2", [lambda: P.matmul(ps[7][:, 0:NS], T.bd[:], T.xx[:], True, True)], ["xx", "bd"])
+    before = {0: "S_0"}
+    between = [
+        [("yy", lambda: V.tensor_tensor(T.yy[:], ps[7][:, 0:NS], T.diag[:], Alu.mult), ["e2"])],
+        [("zz", lambda: V.tensor_tensor_scan(T.zz[:], T.nf[:], T.yy[:], 0.0, Alu.mult, Alu.add), ["yy", "nf"])],
+        [("t3", lambda: V.tensor_tensor(T.t3[:], T.zz[:, 15:NS:16], T.k2[:], Alu.mult), ["zz", "k2"]),
+         ("off", lambda: V.tensor_copy(T.off[:], T.t2[:]), ["t2"])],
+        [("t4", lambda: V.tensor_tensor(T.t4[:], T.t3[:], T.zz[:, 15:NS:16], Alu.min), ["t3"]),
+         ("offs", lambda: V.tensor_scalar(T.offs[:], T.t4[:], float(H0), None, Alu.add), ["t4"])],
+    ]
+    for k, (a, b, pair) in enumerate(first):
+        if k > 0:
+            old = before.get(pair)
+            mm1("B%d_0" % k, 2 * pair, T.bendb, T.fl[:, a:b], b - a, ["Q" + old] if old else [])
+            mm1("A%d_0" % k, 2 * pair + 1, T.mixb, T.fl[:, a:b], b - a, ["D" + old] if old else [])
+        before[pair] = "%d_0" % k
+        square("Q%d_0" % k, T.sq[:, a:b], pair, b - a, ["B%d_0" % k])
+        for name, emit, deps in between[k]:
+            put("D", name, [emit], deps)
+        total("D%d_0" % k, W[0][:, H0 + a:H0 + b], pair, b - a, T.sq[:, a:b], ["A%d_0" % k, "Q%d_0" % k])
+        swap(0, k, a, b, ["D%d_0" % k])
+    done = ["D%d_0" % k for k in range(len(first))]
+    opps = [(b, ["op%d_0" % k]) for k, (a, b, pair) in enumerate(first)]
+
+    def window(t, a, b, done, opps):
+        deps = done + ["arr%d" % t, "own%d" % t, "off"]
+        lo = 0
+        for end, names in opps:
+            if lo < b:
+                deps = deps + names
+            lo = end
+        return W[t][:, H0:O0 + b].indirect(T.off[:, a // 16:b // 16]), deps
+
+    def copy(q, name, out, src, deps):
+        if q == "A":
+            put(q, name, [lambda: A.activation(out, src, Act.Copy)], deps)
+        else:
+            put(q, name, [lambda: V.tensor_copy(out, src)], deps)
+
+    span, at = {}, 0
+    for name, n, mode, pair in CHUNKS:
+        span[name] = (at, at + n, mode, pair)
+        at += n
+    users = {0: ["S"]}
+    for name, n, mode, pair in CHUNKS:
+        users.setdefault(pair, []).append(name)
+    for t in range(1, STEPS):
+        tag = "_%d" % t
+        for q in "ADP":
+            for o in ORDER[q]:
+                kind, c = o[0], o[1:]
+                if c[0] == "S":
+                    if kind == "G":
+                        a, b = (0, S) if c == "S0" else (S, NS)
+                        copy(q, o + tag, T.vs[:, a:b], W[t - 1][:, 0:A0].indirect(T.offs[:, a // 16:b // 16]),
+                             done + ["opS_%d" % (t - 1), "offs"])
+                    elif kind in "BA":
+                        a, b = (0, S) if c == "S0" else (S, NS)
+                        w, bank = (T.bendf, 0) if kind == "B" else (T.mixf, 1)
+                        put(q, o + tag, [lambda a=a, b=b, w=w, bank=bank: P.matmul(ps[bank][:, a:b], w[:], T.vs[:, a:b], True, True)],
+                            ["G" + c + tag, "bendf", "mixf"])
+                    elif kind == "Q":
+                        square(o + tag, T.sqs[:], 0, NS, ["BS0" + tag, "BS1" + tag])
+                    else:
+                        total(o + tag, T.hs[:, t * NS:(t + 1) * NS], 0, NS, T.sqs[:], ["AS0" + tag, "AS1" + tag, "QS" + tag])
+                    continue
+                a, b, mode, pair = span[c]
+                n = b - a
+                u = users[pair]
+                old = u[u.index(c) - 1] + tag if u.index(c) > 0 else None
+                pb, pa = ps[2 * pair][:, 0:n], ps[2 * pair + 1][:, 0:n]
+                if kind in "GH":
+                    src, deps = window(t - 1, a, b, done, opps)
+                    copy(q, o + tag, (T.v if kind == "G" else T.hi)[:, a:b], src, deps)
+                elif kind == "R":
+                    src, deps = window(t - 1, a, b, done, opps)
+                    put(q, o + tag, [lambda a=a, b=b, src=src: V.tensor_tensor(T.res[:, a:b], src, T.hi[:, a:b], Alu.subtract)],
+                        deps + ["H" + c + tag])
+                elif kind == "M":
+                    copy(q, o + tag, T.mid[:, a:b], T.res[:, a:b], ["R" + c + tag])
+                elif kind == "L":
+                    put(q, o + tag, [lambda a=a, b=b: V.tensor_tensor(T.lo[:, a:b], T.res[:, a:b], T.mid[:, a:b], Alu.subtract)],
+                        ["M" + c + tag])
+                elif kind in "hm":
+                    x = (T.hi if kind == "h" else T.mid)[:, a:b]
+                    deps = [kind.upper() + c + tag] + (["Q" + old, "D" + old] if old and kind == "h" else [])
+                    put(q, o + tag, [lambda pb=pb, x=x, s=(kind == "h"): P.matmul(pb, T.bendb[:], x, s, False),
+                                     lambda pa=pa, x=x, s=(kind == "h"): P.matmul(pa, T.mixb[:], x, s, False)], deps)
+                elif kind in "BA":
+                    out = pb if kind == "B" else pa
+                    if mode == "x":
+                        w = T.bendb if kind == "B" else T.mixb
+                        put(q, o + tag, [lambda out=out, w=w, a=a, b=b: P.matmul(out, w[:], T.lo[:, a:b], False, True)], ["L" + c + tag])
+                    else:
+                        w = T.bendf if kind == "B" else T.mixf
+                        deps = ["G" + c + tag] + ([("Q" if kind == "B" else "D") + old] if old else [])
+                        put(q, o + tag, [lambda out=out, w=w, a=a, b=b: P.matmul(out, w[:], T.v[:, a:b], True, True)], deps)
+                elif kind == "Q":
+                    square(o + tag, T.sq[:, a:b], pair, n, ["B" + c + tag])
+                else:
+                    total(o + tag, W[t][:, H0 + a:H0 + b], pair, n, T.sq[:, a:b], ["A" + c + tag, "Q" + c + tag])
+        send(t)
+        last = t == STEPS - 1
+        opps = []
+        for k, group in enumerate(SWAPS):
+            if group == ["S"]:
+                if not last:
+                    swap_sent(t)
+                continue
+            a, b = span[group[0]][0], span[group[-1]][1]
+            if last and k == len(SWAPS) - 1:
+                opps.append((b, ["X0", "X1"]))
+            else:
+                swap(t, k, a, b, ["D" + c + tag for c in group])
+                opps.append((b, ["op%d_%d" % (k, t)]))
+        done = ["D" + x[0] + tag for x in CHUNKS]
+
+    t = STEPS - 1
+    for q in LAST:
+        for kind, a, b in LAST[q]:
+            if kind == "X":
+                out, src = halves(t, span[SWAPS[-1][0]][0], C)[a]
+                copy(q, "X%d" % a, out, src, done)
+            else:
+                src, deps = window(t, a, b, done, opps)
+                copy(q, "F%d" % a, T.v[:, a:b], src, deps)
+    for k, (a, b) in enumerate(STORES):
+        dma("S", "st%d" % k, [(T.y[:, a:b], T.v[:, a:b])],
+            ["F%d" % x[1] for q in LAST for x in LAST[q] if x[0] == "F" and a <= x[1] < b], "stored")
+
+    token, count = dict(outside), {}
+    for q in calls:
+        for name, emit, deps, sem, inc in calls[q]:
+            count[sem] = count.get(sem, 0) + inc * len(emit)
+            token[name] = (sem, count[sem])
+    for name in outside:
+        count[outside[name][0]] = outside[name][1]
+    clock = {name: (0, {outside[name][0]: outside[name][1]}) for name in outside}
+    known = {q: {} for q in calls}
+    waited = {}
+    pos = {q: 0 for q in calls}
+    serial = 0
+    left = sum(len(calls[q]) for q in calls)
+    while left:
+        moved = False
+        for q in calls:
+            while pos[q] < len(calls[q]):
+                name, emit, deps, sem, inc = calls[q][pos[q]]
+                if any(d not in clock for d in deps):
+                    break
+                for d in sorted(set(deps), key=lambda d: (-clock[d][0], d)):
+                    s, val = token[d]
+                    if known[q].get(s, 0) < val:
+                        queue[q].wait_ge(T.sem[s], val)
+                        waited[s] = max(waited.get(s, 0), val)
+                        for s2, v2 in clock[d][1].items():
+                            known[q][s2] = max(known[q].get(s2, 0), v2)
+                for e in emit:
+                    ins = e()
+                    if ins is not None:
+                        ins.then_inc(T.sem[sem], inc)
+                serial += 1
+                seen = dict(known[q])
+                seen[sem] = token[name][1]
+                clock[name] = (serial, seen)
+                pos[q] += 1
+                left -= 1
+                moved = True
+        assert moved
+    for s in sorted(count, key=lambda s: s == "stored"):
+        if waited.get(s, 0) < count[s]:
+            g.wait_ge(T.sem[s], count[s])

@@ -8,18 +8,19 @@ A0 = H0 + C
 O0 = A0 + N * S
 WL = O0 + C
 
-CHUNKS = [("0", 512, "f", 1), ("1", 288, "x", 2), ("2", 512, "f", 3), ("3", 384, "x", 0), ("4", 224, "f", 1), ("5", 128, "f", 2)]
+CHUNKS = [("0", 320, "x"), ("1", 384, "f"), ("2", 256, "x"), ("3", 448, "f"), ("4", 320, "x"), ("5", 192, "x"), ("6", 128, "f")]
 ORDER = {
-    "A": ["G0", "QS", "G2", "H3", "Q0", "Q1", "M3", "Q2", "G4", "G5", "Q3", "Q4", "Q5"],
-    "D": ["GS0", "GS1", "H1", "DS", "R1", "M1", "L1", "R3", "D0", "D1", "L3", "D2", "D3", "D4", "D5"],
-    "P": ["BS0", "AS0", "BS1", "AS1", "h1", "B0", "A0", "m1", "B1", "A1", "h3", "B2", "A2", "m3", "B3", "A3", "B4", "A4", "B5", "A5"],
+    "A": "GS0 GS1 G1 QS G3 H4 M2 Q1 H5 G6 Q0 Q2 Q3 Q4 Q5 Q6".split(),
+    "D": "H0 R0 H2 DS R2 L0 R4 L2 D1 R5 D0 L4 L5 D2 D3 D4 D5 D6".split(),
+    "P": ("BS0 AS0 BS1 h0 i0 AS1 A1 h2 B1 B3 m0 i2 n0 B0 A0 n2 h4 A2 m2 B2 m4 A3 h5 i4 B4 i5 m5 n4 B5 A4 B6 n5 A5 A6").split(),
+    "G": "M0 T M4 M5".split(),
 }
-SWAPS = [["0"], ["S"], ["1"], ["2"], ["3"], ["4", "5"]]
+SWAPS = [["S"], ["1"], ["0"], ["2"], ["3"], ["4"], ["5", "6"]]
 LAST = {
     "A": [("F", 128, 256), ("F", 512, 800), ("F", 1056, 1312), ("X", 0, 0), ("X", 1, 0), ("F", 1888, 2048)],
-    "D": [("F", 0, 128), ("F", 256, 512), ("F", 800, 1056), ("F", 1312, 1696), ("F", 1696, 1888)],
+    "D": [("F", 0, 128), ("F", 256, 512), ("F", 800, 1056), ("F", 1312, 1728), ("F", 1728, 1888)],
 }
-STORES = [(0, 256), (256, 800), (800, 1312), (1312, 1696), (1696, 2048)]
+STORES = [(0, 256), (256, 800), (800, 1312), (1312, 1728), (1728, 2048)]
 
 SCRATCH = {
     "fl": ("sbuf", [128, C], "bfloat16"), "fs": ("sbuf", [128, NS], "bfloat16"),
@@ -134,11 +135,11 @@ def rank_program(g, core, T, topo):
         dma("S", "opS_%d" % t, [(W[t][0:64, 0:NS], T.hs[64:128, j:j + NS]), (W[t][64:128, 0:NS], T.hs[0:64, j:j + NS])],
             ["DS_%d" % t], "op%d_7" % t)
 
-    def square(name, out, pair, n, deps):
-        put("A", name, [lambda: A.activation(out, ps[2 * pair][:, 0:n], Act.Square, scale=root8)], deps)
+    def square(name, out, bank, n, deps):
+        put("A", name, [lambda: A.activation(out, ps[bank][:, 0:n], Act.Square, scale=root8)], deps)
 
-    def total(name, out, pair, n, sq, deps):
-        put("D", name, [lambda: V.tensor_tensor(out, ps[2 * pair + 1][:, 0:n], sq, Alu.add)], deps)
+    def total(name, out, bank, n, sq, deps):
+        put("D", name, [lambda: V.tensor_tensor(out, ps[bank][:, 0:n], sq, Alu.add)], deps)
 
     def mm1(name, bank, w, rhs, n, deps):
         put("P", name, [lambda: P.matmul(ps[bank][:, 0:n], w[:], rhs, True, True)], deps)
@@ -150,7 +151,7 @@ def rank_program(g, core, T, topo):
     mm1("AS_0", 1, T.mixb, T.fs[:], NS, [])
     mm1("A0_0", 3, T.mixb, T.fl[:, 0:512], 512, [])
     square("QS_0", T.sqs[:], 0, NS, ["BS_0"])
-    total("DS_0", T.hs[:, 0:NS], 0, NS, T.sqs[:], ["AS_0", "QS_0"])
+    total("DS_0", T.hs[:, 0:NS], 1, NS, T.sqs[:], ["AS_0", "QS_0"])
     send(0)
     swap_sent(0)
     put("P", "e2", [lambda: P.matmul(ps[7][:, 0:NS], T.bd[:], T.xx[:], True, True)], ["xx", "bd"])
@@ -169,10 +170,10 @@ def rank_program(g, core, T, topo):
             mm1("B%d_0" % k, 2 * pair, T.bendb, T.fl[:, a:b], b - a, ["Q" + old] if old else [])
             mm1("A%d_0" % k, 2 * pair + 1, T.mixb, T.fl[:, a:b], b - a, ["D" + old] if old else [])
         before[pair] = "%d_0" % k
-        square("Q%d_0" % k, T.sq[:, a:b], pair, b - a, ["B%d_0" % k])
+        square("Q%d_0" % k, T.sq[:, a:b], 2 * pair, b - a, ["B%d_0" % k])
         for name, emit, deps in between[k]:
             put("D", name, [emit], deps)
-        total("D%d_0" % k, W[0][:, H0 + a:H0 + b], pair, b - a, T.sq[:, a:b], ["A%d_0" % k, "Q%d_0" % k])
+        total("D%d_0" % k, W[0][:, H0 + a:H0 + b], 2 * pair + 1, b - a, T.sq[:, a:b], ["A%d_0" % k, "Q%d_0" % k])
         swap(0, k, a, b, ["D%d_0" % k])
     done = ["D%d_0" % k for k in range(len(first))]
     opps = [(b, ["op%d_0" % k]) for k, (a, b, pair) in enumerate(first)]
@@ -193,17 +194,24 @@ def rank_program(g, core, T, topo):
             put(q, name, [lambda: V.tensor_copy(out, src)], deps)
 
     span, at = {}, 0
-    for name, n, mode, pair in CHUNKS:
-        span[name] = (at, at + n, mode, pair)
+    for name, n, mode in CHUNKS:
+        span[name] = (at, at + n, mode)
         at += n
-    users = {0: ["S"]}
-    for name, n, mode, pair in CHUNKS:
-        users.setdefault(pair, []).append(name)
+    bank_of, emptied, reader = {}, {}, [None] * 8
+    for o in ORDER["P"]:
+        key = ("B" if o[0] in "hmB" else "A") + o[1]
+        if key not in bank_of:
+            k = len(bank_of) % 8
+            bank_of[key], emptied[o] = k, reader[k]
+            reader[k] = ("Q" if key[0] == "B" else "D") + o[1]
     for t in range(1, STEPS):
         tag = "_%d" % t
-        for q in "ADP":
+        for q in "ADPG":
             for o in ORDER[q]:
                 kind, c = o[0], o[1:]
+                if o == "T":
+                    send(t)
+                    continue
                 if c[0] == "S":
                     if kind == "G":
                         a, b = (0, S) if c == "S0" else (S, NS)
@@ -211,20 +219,31 @@ def rank_program(g, core, T, topo):
                              done + ["opS_%d" % (t - 1), "offs"])
                     elif kind in "BA":
                         a, b = (0, S) if c == "S0" else (S, NS)
-                        w, bank = (T.bendf, 0) if kind == "B" else (T.mixf, 1)
+                        w, bank = (T.bendf if kind == "B" else T.mixf), bank_of[kind + "S"]
                         put(q, o + tag, [lambda a=a, b=b, w=w, bank=bank: P.matmul(ps[bank][:, a:b], w[:], T.vs[:, a:b], True, True)],
                             ["G" + c + tag, "bendf", "mixf"])
                     elif kind == "Q":
-                        square(o + tag, T.sqs[:], 0, NS, ["BS0" + tag, "BS1" + tag])
+                        square(o + tag, T.sqs[:], bank_of["BS"], NS, ["BS0" + tag, "BS1" + tag])
                     else:
-                        total(o + tag, T.hs[:, t * NS:(t + 1) * NS], 0, NS, T.sqs[:], ["AS0" + tag, "AS1" + tag, "QS" + tag])
+                        total(o + tag, T.hs[:, t * NS:(t + 1) * NS], bank_of["AS"], NS, T.sqs[:],
+                              ["AS0" + tag, "AS1" + tag, "QS" + tag])
                     continue
-                a, b, mode, pair = span[c]
+                a, b, mode = span[c]
                 n = b - a
-                u = users[pair]
-                old = u[u.index(c) - 1] + tag if u.index(c) > 0 else None
-                pb, pa = ps[2 * pair][:, 0:n], ps[2 * pair + 1][:, 0:n]
-                if kind in "GH":
+                if q == "P":
+                    side = "B" if kind in "hmB" else "A"
+                    if mode == "f":
+                        x, w, src = T.v, (T.bendf if side == "B" else T.mixf), "G"
+                    else:
+                        x, src = {"h": (T.hi, "H"), "i": (T.hi, "H"), "m": (T.mid, "M"), "n": (T.mid, "M")}.get(kind, (T.lo, "L"))
+                        w = T.bendb if side == "B" else T.mixb
+                    out, first_, last_ = ps[bank_of[side + c]][:, 0:n], o in emptied, kind in "BA"
+                    put(q, o + tag, [lambda out=out, w=w, x=x[:, a:b], s=first_, e=last_: P.matmul(out, w[:], x, s, e)],
+                        [src + c + tag] + ([emptied[o] + tag] if emptied.get(o) else []))
+                elif q == "G":
+                    put(q, o + tag, [lambda a=a, b=b: g.affine_select(T.mid[:, a:b], T.res[:, a:b], [[0, b - a]], Alu.is_ge, 0.0, 0, 0)],
+                        ["R" + c + tag])
+                elif kind in "GH":
                     src, deps = window(t - 1, a, b, done, opps)
                     copy(q, o + tag, (T.v if kind == "G" else T.hi)[:, a:b], src, deps)
                 elif kind == "R":
@@ -236,25 +255,10 @@ def rank_program(g, core, T, topo):
                 elif kind == "L":
                     put(q, o + tag, [lambda a=a, b=b: V.tensor_tensor(T.lo[:, a:b], T.res[:, a:b], T.mid[:, a:b], Alu.subtract)],
                         ["M" + c + tag])
-                elif kind in "hm":
-                    x = (T.hi if kind == "h" else T.mid)[:, a:b]
-                    deps = [kind.upper() + c + tag] + (["Q" + old, "D" + old] if old and kind == "h" else [])
-                    put(q, o + tag, [lambda pb=pb, x=x, s=(kind == "h"): P.matmul(pb, T.bendb[:], x, s, False),
-                                     lambda pa=pa, x=x, s=(kind == "h"): P.matmul(pa, T.mixb[:], x, s, False)], deps)
-                elif kind in "BA":
-                    out = pb if kind == "B" else pa
-                    if mode == "x":
-                        w = T.bendb if kind == "B" else T.mixb
-                        put(q, o + tag, [lambda out=out, w=w, a=a, b=b: P.matmul(out, w[:], T.lo[:, a:b], False, True)], ["L" + c + tag])
-                    else:
-                        w = T.bendf if kind == "B" else T.mixf
-                        deps = ["G" + c + tag] + ([("Q" if kind == "B" else "D") + old] if old else [])
-                        put(q, o + tag, [lambda out=out, w=w, a=a, b=b: P.matmul(out, w[:], T.v[:, a:b], True, True)], deps)
                 elif kind == "Q":
-                    square(o + tag, T.sq[:, a:b], pair, n, ["B" + c + tag])
+                    square(o + tag, T.sq[:, a:b], bank_of["B" + c], n, ["B" + c + tag])
                 else:
-                    total(o + tag, W[t][:, H0 + a:H0 + b], pair, n, T.sq[:, a:b], ["A" + c + tag, "Q" + c + tag])
-        send(t)
+                    total(o + tag, W[t][:, H0 + a:H0 + b], bank_of["A" + c], n, T.sq[:, a:b], ["A" + c + tag, "Q" + c + tag])
         last = t == STEPS - 1
         opps = []
         for k, group in enumerate(SWAPS):
@@ -268,6 +272,7 @@ def rank_program(g, core, T, topo):
             else:
                 swap(t, k, a, b, ["D" + c + tag for c in group])
                 opps.append((b, ["op%d_%d" % (k, t)]))
+        opps.sort()
         done = ["D" + x[0] + tag for x in CHUNKS]
 
     t = STEPS - 1

@@ -7,20 +7,31 @@ H0 = NS
 A0 = H0 + C
 O0 = A0 + N * S
 WL = O0 + C
+BIG = 4096.0
 
-CHUNKS = [("0", 320, "x"), ("1", 384, "f"), ("2", 256, "x"), ("3", 448, "f"), ("4", 320, "x"), ("5", 192, "x"), ("6", 128, "f")]
+FIRST = [384, 384, 384, 448, 448]
+HOLD = 9
+START = {
+    "A": "nf0 nf big GS0 mk QS Q0 Q1 Q2 Q3 Q4".split(),
+    "D": "ones dj own0 diag pm own1 s_hi s_lo sf kn k2 su GS1 t1 t2 xx DS off D0 zz t3 D1 t4 offs D2 D3 D4".split(),
+    "P": "rep e1 B0 BS AS B1 A0 e2 B2 A1 B3 A2 B4 A3 A4".split(),
+    "G": "di sel k0 bd0 bd bendf mixf T XS own2 own3 own4 own5".split(),
+}
+CHUNKS = [("0", 352, "f"), ("1", 416, "f"), ("2", 352, "z"), ("3", 448, "z"), ("4", 288, "x"), ("5", 128, "x"), ("6", 64, "f")]
 ORDER = {
-    "A": "GS0 GS1 G1 QS G3 H4 M2 Q1 H5 G6 Q0 Q2 Q3 Q4 Q5 Q6".split(),
-    "D": "H0 R0 H2 DS R2 L0 R4 L2 D1 R5 D0 L4 L5 D2 D3 D4 D5 D6".split(),
-    "P": ("BS0 AS0 BS1 h0 i0 AS1 A1 h2 B1 B3 m0 i2 n0 B0 A0 n2 h4 A2 m2 B2 m4 A3 h5 i4 B4 i5 m5 n4 B5 A4 B6 n5 A5 A6").split(),
-    "G": "M0 T M4 M5".split(),
+    "A": "GS1 G1 QS H3 H4 C2 Q1 H5 Q0 C3 M4 M5 G6 Q2 Q3 Q4 Q5 Q6".split(),
+    "D": "GS0 G0 H2 DS R2 R3 R4 L2 R5 D0 L3 L4 D1 L5 D2 D3 D4 D5 D6".split(),
+    "P": "BS0 BS1 AS0 AS1 A0 B1 B0 A1 h3 h2 h4 m2 i2 n2 B2 m3 A2 h5 m4 m5 B3 i3 n3 B4 A3 i4 n4 B5 A4 B6 i5 n5 A5 A6".split(),
+    "G": "T M2 M3".split(),
 }
-SWAPS = [["S"], ["1"], ["0"], ["2"], ["3"], ["4"], ["5", "6"]]
+SWAPS = [["S"], ["0"], ["1"], ["2"], ["3"], ["4"], ["5", "6"]]
 LAST = {
-    "A": [("F", 128, 256), ("F", 512, 800), ("F", 1056, 1312), ("X", 0, 0), ("X", 1, 0), ("F", 1888, 2048)],
-    "D": [("F", 0, 128), ("F", 256, 512), ("F", 800, 1056), ("F", 1312, 1728), ("F", 1728, 1888)],
+    "A": [("F", 128, 256), ("F", 448, 768), ("X", 0, "6"), ("F", 960, 1120), ("F", 1344, 1568), ("F", 1728, 1856), ("F", 1952, 2048)],
+    "D": [("F", 0, 128), ("F", 256, 448), ("X", 1, "6"), ("F", 768, 960), ("F", 1120, 1344), ("F", 1568, 1728), ("F", 1856, 1952)],
+    "G": [("X", 0, "5"), ("X", 1, "5")],
 }
-STORES = [(0, 256), (256, 800), (800, 1312), (1312, 1728), (1728, 2048)]
+BY_ENGINE = ["5"]
+STORES = [(0, 256), (256, 768), (768, 1120), (1120, 1568), (1568, 1856), (1856, 2048)]
 
 SCRATCH = {
     "fl": ("sbuf", [128, C], "bfloat16"), "fs": ("sbuf", [128, NS], "bfloat16"),
@@ -32,12 +43,12 @@ SCRATCH = {
     "sq": ("sbuf", [128, C], "float32"), "sqs": ("sbuf", [128, NS], "float32"),
     "lk": ("sbuf", [128, 128], "int32"), "si": ("sbuf", [128, 36], "int32"), "sf": ("sbuf", [128, 36], "float32"),
     "su": ("sbuf", [128, 36], "uint16"), "off": ("sbuf", [128, 128], "uint16"), "offs": ("sbuf", [128, 12], "uint16"),
-    "di": ("sbuf", [128, NS], "int32"), "dj": ("sbuf", [128, NS], "int32"), "diag": ("sbuf", [128, NS], "float32"),
-    "pm": ("sbuf", [128, 4], "float32"), "k0": ("sbuf", [128, 128], "float32"), "kn": ("sbuf", [128, 128], "float32"),
-    "k2": ("sbuf", [128, 12], "float32"), "ones": ("sbuf", [128, 128], "float32"), "bd0": ("sbuf", [128, 128], "float32"),
+    "di": ("sbuf", [128, 16], "int32"), "dj": ("sbuf", [128, 16], "int32"), "diag": ("sbuf", [128, 16], "float32"),
+    "pm": ("sbuf", [128, 4], "float32"), "k0": ("sbuf", [128, 128], "float32"), "ones": ("sbuf", [128, NS], "float32"),
+    "k2": ("sbuf", [128, 12], "float32"), "bd0": ("sbuf", [128, 128], "float32"),
     "bd": ("sbuf", [128, 128], "float32"), "nf": ("sbuf", [128, NS], "float32"), "mk": ("sbuf", [128, NS], "float32"),
-    "xx": ("sbuf", [128, NS], "float32"), "yy": ("sbuf", [128, NS], "float32"), "zz": ("sbuf", [128, NS], "float32"),
-    "t1": ("sbuf", [128, 128], "float32"), "t2": ("sbuf", [128, 128], "float32"),
+    "xx": ("sbuf", [128, NS], "float32"), "big": ("sbuf", [128, 128], "float32"), "zz": ("sbuf", [128, NS], "float32"),
+    "sel": ("sbuf", [128, NS], "float32"), "t2": ("sbuf", [128, 128], "float32"),
     "t3": ("sbuf", [128, 12], "float32"), "t4": ("sbuf", [128, 12], "float32"),
 }
 for _t in range(STEPS):
@@ -45,9 +56,22 @@ for _t in range(STEPS):
 for _b in range(8):
     SCRATCH["ps%d" % _b] = ("psum", [128, 512], "float32")
 
-SEMAPHORES = (["cA", "cD", "cP", "cG", "lds", "ldf", "ldl", "ldw", "sent", "stored"]
+SEMAPHORES = (["cA", "cD", "cP", "cG", "lds", "ldr", "ldf", "ldl", "ldb", "ldm", "sent", "stored"]
               + ["arr%d" % t for t in range(STEPS)]
               + ["op%d_%d" % (t, k) for t in range(STEPS) for k in range(8)])
+
+
+def banks(order, count):
+    bank_of, emptied, reader = {}, {}, [None] * count
+    for o in order:
+        if o[0] not in "hmBinA":
+            continue
+        key = ("B" if o[0] in "hmB" else "A") + o[1]
+        if key not in bank_of:
+            k = len(bank_of) % count
+            bank_of[key], emptied[o] = k, reader[k]
+            reader[k] = ("Q" if key[0] == "B" else "D") + o[1]
+    return bank_of, emptied
 
 
 def rank_program(g, core, T, topo):
@@ -68,72 +92,16 @@ def rank_program(g, core, T, topo):
     ps = [T["ps%d" % b] for b in range(8)]
     V, A, P = g.vector, g.scalar, g.tensor
     others = [r for r in range(N) if r != rank]
+    own = A0 + rank * S
     root8 = 0.125 ** 0.5
 
-    pieces = []
-    if rank > 0:
-        pieces.append((T.si[0:16, 0:4 * rank], T.sends[:, 0:4 * rank]))
-    if rank < N - 1:
-        pieces.append((T.si[0:16, 4 * rank:12], T.sends[:, 4 * rank + 4:16]))
-    dma("A", "ld_s", pieces, [], "lds")
-    dma("A", "ld_l", [(T.lk[:], T.links[:])], [], "ldl")
-    dma("S", "ld_f", [(T.fl[:], T.flow[:])], [], "ldf")
-    dma("S", "ld_w", [(T.bendb[:], T.bend[:]), (T.mixb[:], T.mix[:])], [], "ldw")
-
-    put("G", "di", [lambda: g.iota(T.di[:], [[0, 12], [-1, 16]], 16, 1)])
-    put("G", "k0", [lambda: g.iota(T.k0[:], [[-16, 128]], -(O0 - H0), 0, allow_small_or_imprecise_dtypes=True)])
-    put("G", "ones", [lambda: g.iota(T.ones[:], [[0, 128]], 1, 0, allow_small_or_imprecise_dtypes=True)])
-    put("G", "bd0", [lambda: g.affine_select(T.bd0[:], T.ones[:], [[-16, 8], [0, 16]], Alu.is_ge, 0.0, 0, 1)], ["ones"])
-    put("G", "bd", [lambda: g.affine_select(T.bd[:], T.bd0[:], [[16, 8], [0, 16]], Alu.is_ge, 0.0, 15, -1)], ["bd0"])
-    own = A0 + rank * S
-    for t in range(STEPS):
-        put("D", "own%d" % t, [lambda t=t: V.memset(W[t][:, own:own + S], 0.0)])
-    put("D", "nf0", [lambda: V.memset(T.nf[:], 1.0)])
-    put("D", "dj", [lambda: V.tensor_scalar(T.dj[:], T.di[:], 15, None, Alu.bitwise_and)], ["di"])
-    put("D", "nf", [lambda: V.memset(T.nf[:, 0:NS:16], 0.0)], ["nf0"])
-    put("D", "diag", [lambda: V.tensor_scalar(T.diag[:], T.dj[:], 0.0, None, Alu.is_equal)], ["dj"])
-    put("D", "pm", [lambda: V.tensor_copy(T.pm[:, 0:1], T.dj[:, 0:1])], ["dj"])
-    put("D", "kn", [lambda: V.tensor_scalar(T.kn[:], T.k0[:], T.pm[:, 0:1], None, Alu.subtract)], ["pm", "k0"])
-    put("D", "k2", [lambda: V.tensor_scalar(T.k2[:], T.kn[:, 0:12], float(O0), None, Alu.add)], ["kn"])
-
-    put("D", "s_hi", [lambda: V.tensor_scalar(T.si[0:16, 12:24], T.si[0:16, 0:12], 4, None, Alu.arith_shift_right)], ["ld_s"])
-    put("D", "s_lo", [lambda: V.tensor_scalar(T.si[0:16, 24:36], T.si[0:16, 0:12], 15, None, Alu.bitwise_and)], ["ld_s"])
-    put("D", "sf", [lambda: V.tensor_copy(T.sf[0:16, :], T.si[0:16, :])], ["s_hi", "s_lo"])
-    put("P", "rep", [lambda: P.matmul(ps[6][:, 0:36], T.diag[0:16, 0:128], T.sf[0:16, :], True, True)], ["sf", "diag"])
-    put("D", "su", [lambda: V.tensor_copy(T.su[:], ps[6][:, 0:36])], ["rep"])
-    put("D", "mk", [lambda: V.tensor_copy(T.mk[:], T.diag[:, 0:16].indirect(T.su[:, 24:36]))], ["su"])
-    put("D", "t1", [lambda: V.tensor_tensor(T.t1[:], T.lk[:], T.kn[:], Alu.mult)], ["ld_l", "kn"])
-    put("D", "xx", [lambda: V.tensor_tensor(T.xx[:], T.lk[:, 0:128].indirect(T.su[:, 12:24]), T.mk[:], Alu.mult)], ["mk", "ld_l"])
-    put("D", "t2", [lambda: V.tensor_tensor(T.t2[:], T.t1[:], T.lk[:], Alu.max)], ["t1"])
-    put("A", "bendf", [lambda: A.activation(T.bendf[:], T.bendb[:], Act.Copy)], ["ld_w"])
-    put("A", "mixf", [lambda: A.activation(T.mixf[:], T.mixb[:], Act.Copy)], ["ld_w"])
-
-    def send(t):
-        moves = []
-        for d in range(1, N):
-            r = (rank + d) % N
-            dst = T.cores[r]
-            eng = topo.engines(core, dst)
-            pick = [eng[0::2], eng[1::2], eng][d - 1]
-            rid, pid = topo.addr(dst)[0:2]
-            j = t * NS + others.index(r) * S
-            moves.append(RemoteDMATransfer(dst_ids=[DstId(rid=rid, pnc=pid)], dma_engine_mask=sum(1 << e for e in pick),
-                                           remote_sem=T.sem["arr%d" % t], src=T.hs[:, j:j + S], dst=W[t][:, own:own + S]))
-        n = len(topo.engines(core, T.cores[others[0]]))
-        outside["arr%d" % t] = ("arr%d" % t, 2 * n)
-        put("G", "send%d" % t, [lambda: (g.remote_dma_fused(moves[0:2], local_sem=T.sem.sent), None)[1],
-                                lambda: (g.remote_dma_fused(moves[2:3], local_sem=T.sem.sent), None)[1]], ["DS_%d" % t], "sent", n)
-
-    def halves(t, a, b):
-        return [(W[t][0:64, O0 + a:O0 + b], W[t][64:128, H0 + a:H0 + b]), (W[t][64:128, O0 + a:O0 + b], W[t][0:64, H0 + a:H0 + b])]
-
-    def swap(t, k, a, b, deps):
-        dma("S", "op%d_%d" % (k, t), halves(t, a, b), deps, "op%d_%d" % (t, k))
-
-    def swap_sent(t):
-        j = t * NS
-        dma("S", "opS_%d" % t, [(W[t][0:64, 0:NS], T.hs[64:128, j:j + NS]), (W[t][64:128, 0:NS], T.hs[0:64, j:j + NS])],
-            ["DS_%d" % t], "op%d_7" % t)
+    def copy(q, name, out, src, deps):
+        if q == "A":
+            put(q, name, [lambda: A.activation(out, src, Act.Copy)], deps)
+        elif q == "D":
+            put(q, name, [lambda: V.tensor_copy(out, src)], deps)
+        else:
+            put(q, name, [lambda: g.affine_select(out, src, [[0, out.shape[1]]], Alu.is_ge, 0.0, 0, 0)], deps)
 
     def square(name, out, bank, n, deps):
         put("A", name, [lambda: A.activation(out, ps[bank][:, 0:n], Act.Square, scale=root8)], deps)
@@ -141,42 +109,32 @@ def rank_program(g, core, T, topo):
     def total(name, out, bank, n, sq, deps):
         put("D", name, [lambda: V.tensor_tensor(out, ps[bank][:, 0:n], sq, Alu.add)], deps)
 
-    def mm1(name, bank, w, rhs, n, deps):
-        put("P", name, [lambda: P.matmul(ps[bank][:, 0:n], w[:], rhs, True, True)], deps)
+    def send(t):
+        moves = []
+        for d in range(1, N):
+            r = (rank + d) % N
+            dst = T.cores[r]
+            eng = topo.engines(core, dst)
+            pick = ([eng[0::2], eng[1::2], eng] if t == 0 else [eng[0::2], eng[1::4], eng[3::4]])[d - 1]
+            rid, pid = topo.addr(dst)[0:2]
+            j = t * NS + others.index(r) * S
+            moves.append(RemoteDMATransfer(dst_ids=[DstId(rid=rid, pnc=pid)], dma_engine_mask=sum(1 << e for e in pick),
+                                           remote_sem=T.sem["arr%d" % t], src=T.hs[:, j:j + S], dst=W[t][:, own:own + S]))
+        n = len(eng)
+        parts = [moves[0:2], moves[2:3]] if t == 0 else [moves]
+        outside["arr%d" % t] = ("arr%d" % t, len(parts) * n)
+        put("G", "send%d" % t, [lambda m=m: (g.remote_dma_fused(m, local_sem=T.sem.sent), None)[1] for m in parts],
+            ["DS_%d" % t], "sent", n)
 
-    put("A", "GS_0", [lambda: A.activation(T.fs[:], T.fl[:, 0:C].indirect(T.su[:, 0:12]), Act.Copy)], ["su", "ld_f"])
-    first = [(0, 512, 1), (512, 1024, 2), (1024, 1536, 0), (1536, 2048, 1)]
-    mm1("B0_0", 2, T.bendb, T.fl[:, 0:512], 512, ["ld_f", "ld_w"])
-    mm1("BS_0", 0, T.bendb, T.fs[:], NS, ["GS_0"])
-    mm1("AS_0", 1, T.mixb, T.fs[:], NS, [])
-    mm1("A0_0", 3, T.mixb, T.fl[:, 0:512], 512, [])
-    square("QS_0", T.sqs[:], 0, NS, ["BS_0"])
-    total("DS_0", T.hs[:, 0:NS], 1, NS, T.sqs[:], ["AS_0", "QS_0"])
-    send(0)
-    swap_sent(0)
-    put("P", "e2", [lambda: P.matmul(ps[7][:, 0:NS], T.bd[:], T.xx[:], True, True)], ["xx", "bd"])
-    before = {0: "S_0"}
-    between = [
-        [("yy", lambda: V.tensor_tensor(T.yy[:], ps[7][:, 0:NS], T.diag[:], Alu.mult), ["e2"])],
-        [("zz", lambda: V.tensor_tensor_scan(T.zz[:], T.nf[:], T.yy[:], 0.0, Alu.mult, Alu.add), ["yy", "nf"])],
-        [("t3", lambda: V.tensor_tensor(T.t3[:], T.zz[:, 15:NS:16], T.k2[:], Alu.mult), ["zz", "k2"]),
-         ("off", lambda: V.tensor_copy(T.off[:], T.t2[:]), ["t2"])],
-        [("t4", lambda: V.tensor_tensor(T.t4[:], T.t3[:], T.zz[:, 15:NS:16], Alu.min), ["t3"]),
-         ("offs", lambda: V.tensor_scalar(T.offs[:], T.t4[:], float(H0), None, Alu.add), ["t4"])],
-    ]
-    for k, (a, b, pair) in enumerate(first):
-        if k > 0:
-            old = before.get(pair)
-            mm1("B%d_0" % k, 2 * pair, T.bendb, T.fl[:, a:b], b - a, ["Q" + old] if old else [])
-            mm1("A%d_0" % k, 2 * pair + 1, T.mixb, T.fl[:, a:b], b - a, ["D" + old] if old else [])
-        before[pair] = "%d_0" % k
-        square("Q%d_0" % k, T.sq[:, a:b], 2 * pair, b - a, ["B%d_0" % k])
-        for name, emit, deps in between[k]:
-            put("D", name, [emit], deps)
-        total("D%d_0" % k, W[0][:, H0 + a:H0 + b], 2 * pair + 1, b - a, T.sq[:, a:b], ["A%d_0" % k, "Q%d_0" % k])
-        swap(0, k, a, b, ["D%d_0" % k])
-    done = ["D%d_0" % k for k in range(len(first))]
-    opps = [(b, ["op%d_0" % k]) for k, (a, b, pair) in enumerate(first)]
+    def halves(t, a, b):
+        return [(W[t][0:64, O0 + a:O0 + b], W[t][64:128, H0 + a:H0 + b]), (W[t][64:128, O0 + a:O0 + b], W[t][0:64, H0 + a:H0 + b])]
+
+    def sent_halves(t):
+        j = t * NS
+        return [(W[t][0:64, 0:NS], T.hs[64:128, j:j + NS]), (W[t][64:128, 0:NS], T.hs[0:64, j:j + NS])]
+
+    def swap(t, k, a, b, deps):
+        dma("S", "op%d_%d" % (k, t), halves(t, a, b), deps, "op%d_%d" % (t, k))
 
     def window(t, a, b, done, opps):
         deps = done + ["arr%d" % t, "own%d" % t, "off"]
@@ -187,23 +145,106 @@ def rank_program(g, core, T, topo):
             lo = end
         return W[t][:, H0:O0 + b].indirect(T.off[:, a // 16:b // 16]), deps
 
-    def copy(q, name, out, src, deps):
-        if q == "A":
-            put(q, name, [lambda: A.activation(out, src, Act.Copy)], deps)
-        else:
-            put(q, name, [lambda: V.tensor_copy(out, src)], deps)
+    pieces = []
+    if rank > 0:
+        pieces.append((T.si[0:16, 0:4 * rank], T.sends[:, 0:4 * rank]))
+    if rank < N - 1:
+        pieces.append((T.si[0:16, 4 * rank:12], T.sends[:, 4 * rank + 4:16]))
+    dma("S", "ld_s", pieces[:1], [], "lds")
+    dma("S", "ld_r", pieces[1:], [], "ldr")
+    dma("S", "ld_f", [(T.fl[:], T.flow[:])], [], "ldf")
+    dma("A", "ld_b", [(T.bendb[:], T.bend[:])], [], "ldb")
+    dma("S", "ld_m", [(T.mixb[:], T.mix[:])], [], "ldm")
+    dma("S", "ld_l", [(T.lk[:], T.links[:])], [], "ldl")
+
+    lists = {
+        "di": (lambda: g.iota(T.di[:], [[-1, 16]], 16, 1), []),
+        "k0": (lambda: g.iota(T.k0[:], [[-16, 128]], -(O0 - H0), 0, allow_small_or_imprecise_dtypes=True), []),
+        "ones": (lambda: V.memset(T.ones[:], 1.0), []),
+        "bd0": (lambda: g.affine_select(T.bd0[:], T.ones[:, 0:128], [[-16, 8], [0, 16]], Alu.is_ge, 0.0, 0, 1), ["ones"]),
+        "bd": (lambda: g.affine_select(T.bd[:], T.bd0[:], [[16, 8], [0, 16]], Alu.is_ge, 0.0, 15, -1), ["bd0"]),
+        "nf0": (lambda: A.activation(T.nf[:], T.ones[:], Act.Copy, scale=0.0), ["ones"]),
+        "nf": (lambda: A.activation(T.nf[:, 0:NS:16], T.ones[:, 0:12], Act.Copy, scale=-2.0 * BIG), ["nf0"]),
+        "sel": (lambda: g.affine_select(T.sel[0:16, :], T.ones[0:16, :], [[0, 12], [1, 16]], Alu.is_equal, 0.0, 0, -1), ["ones"]),
+        "big": (lambda: A.activation(T.big[0:16, :], T.sel[0:16, 0:128], Act.Identity, scale=BIG, bias=-BIG), ["sel"]),
+        "dj": (lambda: V.tensor_scalar(T.dj[:], T.di[:], 15, None, Alu.bitwise_and), ["di"]),
+        "diag": (lambda: V.tensor_scalar(T.diag[:], T.dj[:], 0.0, None, Alu.is_equal), ["dj"]),
+        "pm": (lambda: V.tensor_copy(T.pm[:, 0:1], T.dj[:, 0:1]), ["dj"]),
+        "kn": (lambda: V.tensor_scalar(ps[7][:, 256:384], T.k0[:], T.pm[:, 0:1], None, Alu.subtract), ["pm", "k0"]),
+        "k2": (lambda: V.tensor_scalar(T.k2[:], T.k0[:, 0:12], T.pm[:, 0:1], float(O0), Alu.subtract, Alu.add), ["pm", "k0"]),
+        "s_hi": (lambda: V.tensor_scalar(T.si[0:16, 12:24], T.si[0:16, 0:12], 4, None, Alu.arith_shift_right), ["ld_s", "ld_r"]),
+        "s_lo": (lambda: V.tensor_scalar(T.si[0:16, 24:36], T.si[0:16, 0:12], 15, None, Alu.bitwise_and), ["ld_s", "ld_r"]),
+        "sf": (lambda: V.tensor_copy(T.sf[0:16, :], T.si[0:16, :]), ["s_hi", "s_lo"]),
+        "rep": (lambda: P.matmul(ps[5][:, 0:36], T.sel[0:16, 0:128], T.sf[0:16, :], True, True), ["sf", "sel"]),
+        "su": (lambda: V.tensor_copy(T.su[:], ps[5][:, 0:36]), ["rep"]),
+        "t1": (lambda: V.tensor_tensor(ps[7][:, 384:512], T.lk[:], ps[7][:, 256:384], Alu.mult), ["ld_l", "kn"]),
+        "t2": (lambda: V.tensor_tensor(T.t2[:], ps[7][:, 384:512], T.lk[:], Alu.max), ["t1"]),
+        "off": (lambda: V.tensor_copy(T.off[:], T.t2[:]), ["t2"]),
+        "xx": (lambda: V.tensor_tensor(T.xx[:], T.lk[:, 0:128].indirect(T.su[:, 12:24]), T.mk[:], Alu.mult), ["mk", "ld_l"]),
+        "e1": (lambda: P.matmul(ps[6][:, 64:64 + NS], T.big[0:16, :], T.sel[0:16, :], True, False), ["big"]),
+        "e2": (lambda: P.matmul(ps[6][:, 64:64 + NS], T.bd[:], T.xx[:], False, True), ["xx", "bd"]),
+        "zz": (lambda: V.tensor_tensor_scan(T.zz[:], T.nf[:], ps[6][:, 64:64 + NS], 0.0, Alu.add, Alu.max), ["e2", "nf"]),
+        "t3": (lambda: V.tensor_tensor(T.t3[:], T.zz[:, 15:NS:16], T.k2[:], Alu.mult), ["zz", "k2"]),
+        "t4": (lambda: V.tensor_tensor(T.t4[:], T.t3[:], T.zz[:, 15:NS:16], Alu.min), ["t3"]),
+        "offs": (lambda: V.tensor_scalar(T.offs[:], T.t4[:], float(H0), None, Alu.add), ["t4"]),
+    }
+
+    span = {"S": (0, NS)}
+    for k, n in enumerate(FIRST):
+        span[str(k)] = (sum(FIRST[:k]), sum(FIRST[:k + 1]))
+    bank_of, emptied = banks(START["P"], 6)
+    for q in START:
+        for o in START[q]:
+            kind, c = o[0], o[1:]
+            if o in lists:
+                put(q, o, [lists[o][0]], lists[o][1])
+            elif o in ("bendf", "mixf"):
+                copy(q, o, T[o][:], T[o[:-1] + "b"][:], ["ld_" + o[0]])
+            elif o == "mk":
+                copy(q, o, T.mk[:], T.diag[:, 0:16].indirect(T.su[:, 24:36]), ["su"])
+            elif o[0:3] == "own":
+                slot = W[int(o[3])][:, own:own + S]
+                put(q, o, [(lambda slot=slot: V.memset(slot, 0.0)) if q == "D" else
+                           (lambda slot=slot: g.iota(slot, [[0, S]], 0, 0, allow_small_or_imprecise_dtypes=True))])
+            elif o == "T":
+                send(0)
+            elif kind == "X":
+                pair = sent_halves(0) if c == "S" else halves(0, *span[c])
+                copy(q, o, *pair[0], ["D%s_0" % c, "alone"])
+                copy(q, "op%s_0" % c, *pair[1], [o])
+                put(q, o + "_", [], ["alone"])
+            elif kind == "G":
+                a = int(o[2]) * NS // 2
+                copy(q, o + "_0", T.fs[:, a:a + NS // 2], T.fl[:, 0:C].indirect(T.su[:, a // 16:a // 16 + NS // 32]), ["su", "ld_f"])
+            else:
+                a, b = span[c]
+                sq = T.sqs[:] if c == "S" else T.sq[:, a:b]
+                if kind in "BA":
+                    out, w = ps[bank_of[o]][:, 0:b - a], (T.bendb if kind == "B" else T.mixb)
+                    x = T.fs[:] if c == "S" else T.fl[:, a:b]
+                    put(q, o + "_0", [lambda out=out, w=w, x=x: P.matmul(out, w[:], x, True, True)],
+                        ["ld_" + "bm"[kind == "A"]] + (["GS0_0", "GS1_0"] if c == "S" else ["ld_f"])
+                        + ([emptied[o] + "_0"] if emptied[o] else ["su"] if bank_of[o] == 5 else []))
+                elif kind == "Q":
+                    square(o + "_0", sq, bank_of["B" + c], b - a, ["B" + c + "_0"])
+                else:
+                    out = T.hs[:, 0:NS] if c == "S" else W[0][:, H0 + a:H0 + b]
+                    total(o + "_0", out, bank_of["A" + c], b - a, sq, ["A" + c + "_0", "Q" + c + "_0"])
+                    if "X" + c in START["G"]:
+                        pass
+                    elif c == "S":
+                        dma("S", "opS_0", sent_halves(0), ["DS_0"], "op0_7")
+                    else:
+                        swap(0, int(c), a, b, [o + "_0"] + (["send0"] if int(c) >= HOLD else []))
+    done = ["D%d_0" % k for k in range(len(FIRST))]
+    opps = [(span[str(k)][1], ["op%d_0" % k]) for k in range(len(FIRST))]
 
     span, at = {}, 0
     for name, n, mode in CHUNKS:
         span[name] = (at, at + n, mode)
         at += n
-    bank_of, emptied, reader = {}, {}, [None] * 8
-    for o in ORDER["P"]:
-        key = ("B" if o[0] in "hmB" else "A") + o[1]
-        if key not in bank_of:
-            k = len(bank_of) % 8
-            bank_of[key], emptied[o] = k, reader[k]
-            reader[k] = ("Q" if key[0] == "B" else "D") + o[1]
+    bank_of, emptied = banks(ORDER["P"], 8)
+    late = {}
     for t in range(1, STEPS):
         tag = "_%d" % t
         for q in "ADPG":
@@ -213,12 +254,11 @@ def rank_program(g, core, T, topo):
                     send(t)
                     continue
                 if c[0] == "S":
+                    a, b = (0, S) if c == "S0" else (S, NS)
                     if kind == "G":
-                        a, b = (0, S) if c == "S0" else (S, NS)
                         copy(q, o + tag, T.vs[:, a:b], W[t - 1][:, 0:A0].indirect(T.offs[:, a // 16:b // 16]),
                              done + ["opS_%d" % (t - 1), "offs"])
                     elif kind in "BA":
-                        a, b = (0, S) if c == "S0" else (S, NS)
                         w, bank = (T.bendf if kind == "B" else T.mixf), bank_of[kind + "S"]
                         put(q, o + tag, [lambda a=a, b=b, w=w, bank=bank: P.matmul(ps[bank][:, a:b], w[:], T.vs[:, a:b], True, True)],
                             ["G" + c + tag, "bendf", "mixf"])
@@ -237,12 +277,11 @@ def rank_program(g, core, T, topo):
                     else:
                         x, src = {"h": (T.hi, "H"), "i": (T.hi, "H"), "m": (T.mid, "M"), "n": (T.mid, "M")}.get(kind, (T.lo, "L"))
                         w = T.bendb if side == "B" else T.mixb
-                    out, first_, last_ = ps[bank_of[side + c]][:, 0:n], o in emptied, kind in "BA"
-                    put(q, o + tag, [lambda out=out, w=w, x=x[:, a:b], s=first_, e=last_: P.matmul(out, w[:], x, s, e)],
+                        if mode == "z" and kind == "i":
+                            src = "L"
+                    out, opens, closes = ps[bank_of[side + c]][:, 0:n], o in emptied, kind in "BA"
+                    put(q, o + tag, [lambda out=out, w=w, x=x[:, a:b], s=opens, e=closes: P.matmul(out, w[:], x, s, e)],
                         [src + c + tag] + ([emptied[o] + tag] if emptied.get(o) else []))
-                elif q == "G":
-                    put(q, o + tag, [lambda a=a, b=b: g.affine_select(T.mid[:, a:b], T.res[:, a:b], [[0, b - a]], Alu.is_ge, 0.0, 0, 0)],
-                        ["R" + c + tag])
                 elif kind in "GH":
                     src, deps = window(t - 1, a, b, done, opps)
                     copy(q, o + tag, (T.v if kind == "G" else T.hi)[:, a:b], src, deps)
@@ -252,9 +291,13 @@ def rank_program(g, core, T, topo):
                         deps + ["H" + c + tag])
                 elif kind == "M":
                     copy(q, o + tag, T.mid[:, a:b], T.res[:, a:b], ["R" + c + tag])
+                elif kind == "C":
+                    copy(q, o + tag, ps[bank_of["A" + c]][:, 0:n], T.res[:, a:b],
+                         ["R" + c + tag] + ([emptied["i" + c] + tag] if emptied["i" + c] else []))
                 elif kind == "L":
-                    put(q, o + tag, [lambda a=a, b=b: V.tensor_tensor(T.lo[:, a:b], T.res[:, a:b], T.mid[:, a:b], Alu.subtract)],
-                        ["M" + c + tag])
+                    src = ps[bank_of["A" + c]][:, 0:n] if mode == "z" else T.res[:, a:b]
+                    put(q, o + tag, [lambda a=a, b=b, src=src: V.tensor_tensor(T.lo[:, a:b], src, T.mid[:, a:b], Alu.subtract)],
+                        ["M" + c + tag] + (["C" + c + tag] if mode == "z" else []))
                 elif kind == "Q":
                     square(o + tag, T.sq[:, a:b], bank_of["B" + c], n, ["B" + c + tag])
                 else:
@@ -264,11 +307,13 @@ def rank_program(g, core, T, topo):
         for k, group in enumerate(SWAPS):
             if group == ["S"]:
                 if not last:
-                    swap_sent(t)
+                    dma("S", "opS" + tag, sent_halves(t), ["DS" + tag], "op%d_7" % t)
                 continue
             a, b = span[group[0]][0], span[group[-1]][1]
-            if last and k == len(SWAPS) - 1:
-                opps.append((b, ["X0", "X1"]))
+            if last and group[0] in BY_ENGINE:
+                for c in group:
+                    late[c] = (span[c][0], span[c][1], ["D" + c + tag])
+                    opps.append((span[c][1], ["X0" + c, "X1" + c]))
             else:
                 swap(t, k, a, b, ["D" + c + tag for c in group])
                 opps.append((b, ["op%d_%d" % (k, t)]))
@@ -279,8 +324,8 @@ def rank_program(g, core, T, topo):
     for q in LAST:
         for kind, a, b in LAST[q]:
             if kind == "X":
-                out, src = halves(t, span[SWAPS[-1][0]][0], C)[a]
-                copy(q, "X%d" % a, out, src, done)
+                out, src = halves(t, *late[b][0:2])[a]
+                copy(q, "X%d%s" % (a, b), out, src, late[b][2] + (["alone"] if q == "G" else []))
             else:
                 src, deps = window(t, a, b, done, opps)
                 copy(q, "F%d" % a, T.v[:, a:b], src, deps)
@@ -306,8 +351,11 @@ def rank_program(g, core, T, topo):
         for q in calls:
             while pos[q] < len(calls[q]):
                 name, emit, deps, sem, inc = calls[q][pos[q]]
-                if any(d not in clock for d in deps):
+                if any(d not in clock for d in deps if d != "alone"):
                     break
+                if "alone" in deps:
+                    deps = [d for d in deps if d != "alone"]
+                    g.wait_ge(T.sem.cG, token[name][1] - len(emit))
                 for d in sorted(set(deps), key=lambda d: (-clock[d][0], d)):
                     s, val = token[d]
                     if known[q].get(s, 0) < val:

from concourse.bass import DstId, RemoteDMATransfer
from concourse.mybir import AluOpType as Alu, ActivationFunctionType as Act

C, S, STEPS, N = 2048, 64, 6, 4
NS = (N - 1) * S
H0 = NS
A0 = H0 + C
O0 = A0 + N * S
WL = O0 + C
BIG = 4096.0

FIRST = [384, 384, 384, 448, 448]
HOLD = 9
START = {
    "A": "nf0 nf big GS0 mk QS Q0 Q1 Q2 Q3 Q4".split(),
    "D": "ones dj own0 diag pm own1 s_hi s_lo sf kn k2 su GS1 t1 t2 xx DS off D0 zz t3 D1 t4 offs D2 D3 D4".split(),
    "P": "rep e1 B0 BS AS B1 A0 e2 B2 A1 B3 A2 B4 A3 A4".split(),
    "G": "di sel k0 bd0 bd bendf mixf T XS own2 own3 own4 own5".split(),
}
CHUNKS = [("0", 352, "f"), ("1", 416, "f"), ("2", 352, "z"), ("3", 448, "z"), ("4", 288, "x"), ("5", 128, "x"), ("6", 64, "f")]
ORDER = {
    "A": "GS1 G1 QS H3 H4 C2 Q1 H5 Q0 C3 M4 M5 G6 Q2 Q3 Q4 Q5 Q6".split(),
    "D": "GS0 G0 H2 DS R2 R3 R4 L2 R5 D0 L3 L4 D1 L5 D2 D3 D4 D5 D6".split(),
    "P": "BS0 BS1 AS0 AS1 A0 B1 B0 A1 h3 h2 h4 m2 i2 n2 B2 m3 A2 h5 m4 m5 B3 i3 n3 B4 A3 i4 n4 B5 A4 B6 i5 n5 A5 A6".split(),
    "G": "T M2 M3".split(),
}
SWAPS = [["S"], ["0"], ["1"], ["2"], ["3"], ["4"], ["5", "6"]]
LAST = {
    "A": [("F", 128, 256), ("F", 448, 768), ("X", 0, "6"), ("F", 960, 1120), ("F", 1344, 1568), ("F", 1728, 1856), ("F", 1952, 2048)],
    "D": [("F", 0, 128), ("F", 256, 448), ("X", 1, "6"), ("F", 768, 960), ("F", 1120, 1344), ("F", 1568, 1728), ("F", 1856, 1952)],
    "G": [("X", 0, "5"), ("X", 1, "5")],
}
BY_ENGINE = ["5"]
STORES = [(0, 256), (256, 768), (768, 1120), (1120, 1568), (1568, 1856), (1856, 2048)]

SCRATCH = {
    "fl": ("sbuf", [128, C], "bfloat16"), "fs": ("sbuf", [128, NS], "bfloat16"),
    "mixb": ("sbuf", [128, 128], "bfloat16"), "bendb": ("sbuf", [128, 128], "bfloat16"),
    "mixf": ("sbuf", [128, 128], "float32"), "bendf": ("sbuf", [128, 128], "float32"),
    "hs": ("sbuf", [128, STEPS * NS], "float32"),
    "v": ("sbuf", [128, C], "float32"), "vs": ("sbuf", [128, NS], "float32"), "res": ("sbuf", [128, C], "float32"),
    "hi": ("sbuf", [128, C], "bfloat16"), "mid": ("sbuf", [128, C], "bfloat16"), "lo": ("sbuf", [128, C], "bfloat16"),
    "sq": ("sbuf", [128, C], "float32"), "sqs": ("sbuf", [128, NS], "float32"),
    "lk": ("sbuf", [128, 128], "int32"), "si": ("sbuf", [128, 36], "int32"), "sf": ("sbuf", [128, 36], "float32"),
    "su": ("sbuf", [128, 36], "uint16"), "off": ("sbuf", [128, 128], "uint16"), "offs": ("sbuf", [128, 12], "uint16"),
    "di": ("sbuf", [128, 16], "int32"), "dj": ("sbuf", [128, 16], "int32"), "diag": ("sbuf", [128, 16], "float32"),
    "pm": ("sbuf", [128, 4], "float32"), "k0": ("sbuf", [128, 128], "float32"), "ones": ("sbuf", [128, NS], "float32"),
    "k2": ("sbuf", [128, 12], "float32"), "bd0": ("sbuf", [128, 128], "float32"),
    "bd": ("sbuf", [128, 128], "float32"), "nf": ("sbuf", [128, NS], "float32"), "mk": ("sbuf", [128, NS], "float32"),
    "xx": ("sbuf", [128, NS], "float32"), "big": ("sbuf", [128, 128], "float32"), "zz": ("sbuf", [128, NS], "float32"),
    "sel": ("sbuf", [128, NS], "float32"), "t2": ("sbuf", [128, 128], "float32"),
    "t3": ("sbuf", [128, 12], "float32"), "t4": ("sbuf", [128, 12], "float32"),
}
for _t in range(STEPS):
    SCRATCH["w%d" % _t] = ("sbuf", [128, WL], "float32")
for _b in range(8):
    SCRATCH["ps%d" % _b] = ("psum", [128, 512], "float32")

SEMAPHORES = (["cA", "cD", "cP", "cG", "lds", "ldr", "ldf", "ldl", "ldb", "ldm", "sent", "stored"]
              + ["arr%d" % t for t in range(STEPS)]
              + ["op%d_%d" % (t, k) for t in range(STEPS) for k in range(8)])


def banks(order, count):
    bank_of, emptied, reader = {}, {}, [None] * count
    for o in order:
        if o[0] not in "hmBinA":
            continue
        key = ("B" if o[0] in "hmB" else "A") + o[1]
        if key not in bank_of:
            k = len(bank_of) % count
            bank_of[key], emptied[o] = k, reader[k]
            reader[k] = ("Q" if key[0] == "B" else "D") + o[1]
    return bank_of, emptied


def rank_program(g, core, T, topo):
    rank = T.rank_of(core)
    if rank is None:
        return
    queue = {"A": g.scalar, "D": g.vector, "P": g.tensor, "G": g, "S": g.sync}
    calls = {q: [] for q in queue}
    outside = {}

    def put(q, name, emit, deps=(), sem=None, inc=1):
        calls[q].append((name, emit, list(deps), sem or "c" + q, inc))

    def dma(q, name, pairs, deps, sem):
        put(q, name, [(lambda o=o, i=i: queue[q].dma_start(o, i)) for o, i in pairs], deps, sem, 16)

    W = [T["w%d" % t] for t in range(STEPS)]
    ps = [T["ps%d" % b] for b in range(8)]
    V, A, P = g.vector, g.scalar, g.tensor
    others = [r for r in range(N) if r != rank]
    own = A0 + rank * S
    root8 = 0.125 ** 0.5

    def copy(q, name, out, src, deps):
        if q == "A":
            put(q, name, [lambda: A.activation(out, src, Act.Copy)], deps)
        elif q == "D":
            put(q, name, [lambda: V.tensor_copy(out, src)], deps)
        else:
            put(q, name, [lambda: g.affine_select(out, src, [[0, out.shape[1]]], Alu.is_ge, 0.0, 0, 0)], deps)

    def square(name, out, bank, n, deps):
        put("A", name, [lambda: A.activation(out, ps[bank][:, 0:n], Act.Square, scale=root8)], deps)

    def total(name, out, bank, n, sq, deps):
        put("D", name, [lambda: V.tensor_tensor(out, ps[bank][:, 0:n], sq, Alu.add)], deps)

    def send(t):
        moves = []
        for d in range(1, N):
            r = (rank + d) % N
            dst = T.cores[r]
            eng = topo.engines(core, dst)
            pick = ([eng[0::2], eng[1::2], eng] if t == 0 else [eng[0::2], eng[1::4], eng[3::4]])[d - 1]
            rid, pid = topo.addr(dst)[0:2]
            j = t * NS + others.index(r) * S
            moves.append(RemoteDMATransfer(dst_ids=[DstId(rid=rid, pnc=pid)], dma_engine_mask=sum(1 << e for e in pick),
                                           remote_sem=T.sem["arr%d" % t], src=T.hs[:, j:j + S], dst=W[t][:, own:own + S]))
        n = len(eng)
        parts = [moves[0:2], moves[2:3]] if t == 0 else [moves]
        outside["arr%d" % t] = ("arr%d" % t, len(parts) * n)
        put("G", "send%d" % t, [lambda m=m: (g.remote_dma_fused(m, local_sem=T.sem.sent), None)[1] for m in parts],
            ["DS_%d" % t], "sent", n)

    def halves(t, a, b):
        return [(W[t][0:64, O0 + a:O0 + b], W[t][64:128, H0 + a:H0 + b]), (W[t][64:128, O0 + a:O0 + b], W[t][0:64, H0 + a:H0 + b])]

    def sent_halves(t):
        j = t * NS
        return [(W[t][0:64, 0:NS], T.hs[64:128, j:j + NS]), (W[t][64:128, 0:NS], T.hs[0:64, j:j + NS])]

    def swap(t, k, a, b, deps):
        dma("S", "op%d_%d" % (k, t), halves(t, a, b), deps, "op%d_%d" % (t, k))

    def window(t, a, b, done, opps):
        deps = done + ["arr%d" % t, "own%d" % t, "off"]
        lo = 0
        for end, names in opps:
            if lo < b:
                deps = deps + names
            lo = end
        return W[t][:, H0:O0 + b].indirect(T.off[:, a // 16:b // 16]), deps

    pieces = []
    if rank > 0:
        pieces.append((T.si[0:16, 0:4 * rank], T.sends[:, 0:4 * rank]))
    if rank < N - 1:
        pieces.append((T.si[0:16, 4 * rank:12], T.sends[:, 4 * rank + 4:16]))
    dma("S", "ld_s", pieces[:1], [], "lds")
    dma("S", "ld_r", pieces[1:], [], "ldr")
    dma("S", "ld_f", [(T.fl[:], T.flow[:])], [], "ldf")
    dma("A", "ld_b", [(T.bendb[:], T.bend[:])], [], "ldb")
    dma("S", "ld_m", [(T.mixb[:], T.mix[:])], [], "ldm")
    dma("S", "ld_l", [(T.lk[:], T.links[:])], [], "ldl")

    lists = {
        "di": (lambda: g.iota(T.di[:], [[-1, 16]], 16, 1), []),
        "k0": (lambda: g.iota(T.k0[:], [[-16, 128]], -(O0 - H0), 0, allow_small_or_imprecise_dtypes=True), []),
        "ones": (lambda: V.memset(T.ones[:], 1.0), []),
        "bd0": (lambda: g.affine_select(T.bd0[:], T.ones[:, 0:128], [[-16, 8], [0, 16]], Alu.is_ge, 0.0, 0, 1), ["ones"]),
        "bd": (lambda: g.affine_select(T.bd[:], T.bd0[:], [[16, 8], [0, 16]], Alu.is_ge, 0.0, 15, -1), ["bd0"]),
        "nf0": (lambda: A.activation(T.nf[:], T.ones[:], Act.Copy, scale=0.0), ["ones"]),
        "nf": (lambda: A.activation(T.nf[:, 0:NS:16], T.ones[:, 0:12], Act.Copy, scale=-2.0 * BIG), ["nf0"]),
        "sel": (lambda: g.affine_select(T.sel[0:16, :], T.ones[0:16, :], [[0, 12], [1, 16]], Alu.is_equal, 0.0, 0, -1), ["ones"]),
        "big": (lambda: A.activation(T.big[0:16, :], T.sel[0:16, 0:128], Act.Identity, scale=BIG, bias=-BIG), ["sel"]),
        "dj": (lambda: V.tensor_scalar(T.dj[:], T.di[:], 15, None, Alu.bitwise_and), ["di"]),
        "diag": (lambda: V.tensor_scalar(T.diag[:], T.dj[:], 0.0, None, Alu.is_equal), ["dj"]),
        "pm": (lambda: V.tensor_copy(T.pm[:, 0:1], T.dj[:, 0:1]), ["dj"]),
        "kn": (lambda: V.tensor_scalar(ps[7][:, 256:384], T.k0[:], T.pm[:, 0:1], None, Alu.subtract), ["pm", "k0"]),
        "k2": (lambda: V.tensor_scalar(T.k2[:], T.k0[:, 0:12], T.pm[:, 0:1], float(O0), Alu.subtract, Alu.add), ["pm", "k0"]),
        "s_hi": (lambda: V.tensor_scalar(T.si[0:16, 12:24], T.si[0:16, 0:12], 4, None, Alu.arith_shift_right), ["ld_s", "ld_r"]),
        "s_lo": (lambda: V.tensor_scalar(T.si[0:16, 24:36], T.si[0:16, 0:12], 15, None, Alu.bitwise_and), ["ld_s", "ld_r"]),
        "sf": (lambda: V.tensor_copy(T.sf[0:16, :], T.si[0:16, :]), ["s_hi", "s_lo"]),
        "rep": (lambda: P.matmul(ps[5][:, 0:36], T.sel[0:16, 0:128], T.sf[0:16, :], True, True), ["sf", "sel"]),
        "su": (lambda: V.tensor_copy(T.su[:], ps[5][:, 0:36]), ["rep"]),
        "t1": (lambda: V.tensor_tensor(ps[7][:, 384:512], T.lk[:], ps[7][:, 256:384], Alu.mult), ["ld_l", "kn"]),
        "t2": (lambda: V.tensor_tensor(T.t2[:], ps[7][:, 384:512], T.lk[:], Alu.max), ["t1"]),
        "off": (lambda: V.tensor_copy(T.off[:], T.t2[:]), ["t2"]),
        "xx": (lambda: V.tensor_tensor(T.xx[:], T.lk[:, 0:128].indirect(T.su[:, 12:24]), T.mk[:], Alu.mult), ["mk", "ld_l"]),
        "e1": (lambda: P.matmul(ps[6][:, 64:64 + NS], T.big[0:16, :], T.sel[0:16, :], True, False), ["big"]),
        "e2": (lambda: P.matmul(ps[6][:, 64:64 + NS], T.bd[:], T.xx[:], False, True), ["xx", "bd"]),
        "zz": (lambda: V.tensor_tensor_scan(T.zz[:], T.nf[:], ps[6][:, 64:64 + NS], 0.0, Alu.add, Alu.max), ["e2", "nf"]),
        "t3": (lambda: V.tensor_tensor(T.t3[:], T.zz[:, 15:NS:16], T.k2[:], Alu.mult), ["zz", "k2"]),
        "t4": (lambda: V.tensor_tensor(T.t4[:], T.t3[:], T.zz[:, 15:NS:16], Alu.min), ["t3"]),
        "offs": (lambda: V.tensor_scalar(T.offs[:], T.t4[:], float(H0), None, Alu.add), ["t4"]),
    }

    span = {"S": (0, NS)}
    for k, n in enumerate(FIRST):
        span[str(k)] = (sum(FIRST[:k]), sum(FIRST[:k + 1]))
    bank_of, emptied = banks(START["P"], 6)
    for q in START:
        for o in START[q]:
            kind, c = o[0], o[1:]
            if o in lists:
                put(q, o, [lists[o][0]], lists[o][1])
            elif o in ("bendf", "mixf"):
                copy(q, o, T[o][:], T[o[:-1] + "b"][:], ["ld_" + o[0]])
            elif o == "mk":
                copy(q, o, T.mk[:], T.diag[:, 0:16].indirect(T.su[:, 24:36]), ["su"])
            elif o[0:3] == "own":
                slot = W[int(o[3])][:, own:own + S]
                put(q, o, [(lambda slot=slot: V.memset(slot, 0.0)) if q == "D" else
                           (lambda slot=slot: g.iota(slot, [[0, S]], 0, 0, allow_small_or_imprecise_dtypes=True))])
            elif o == "T":
                send(0)
            elif kind == "X":
                pair = sent_halves(0) if c == "S" else halves(0, *span[c])
                copy(q, o, *pair[0], ["D%s_0" % c, "alone"])
                copy(q, "op%s_0" % c, *pair[1], [o])
                put(q, o + "_", [], ["alone"])
            elif kind == "G":
                a = int(o[2]) * NS // 2
                copy(q, o + "_0", T.fs[:, a:a + NS // 2], T.fl[:, 0:C].indirect(T.su[:, a // 16:a // 16 + NS // 32]), ["su", "ld_f"])
            else:
                a, b = span[c]
                sq = T.sqs[:] if c == "S" else T.sq[:, a:b]
                if kind in "BA":
                    out, w = ps[bank_of[o]][:, 0:b - a], (T.bendb if kind == "B" else T.mixb)
                    x = T.fs[:] if c == "S" else T.fl[:, a:b]
                    put(q, o + "_0", [lambda out=out, w=w, x=x: P.matmul(out, w[:], x, True, True)],
                        ["ld_" + "bm"[kind == "A"]] + (["GS0_0", "GS1_0"] if c == "S" else ["ld_f"])
                        + ([emptied[o] + "_0"] if emptied[o] else ["su"] if bank_of[o] == 5 else []))
                elif kind == "Q":
                    square(o + "_0", sq, bank_of["B" + c], b - a, ["B" + c + "_0"])
                else:
                    out = T.hs[:, 0:NS] if c == "S" else W[0][:, H0 + a:H0 + b]
                    total(o + "_0", out, bank_of["A" + c], b - a, sq, ["A" + c + "_0", "Q" + c + "_0"])
                    if "X" + c in START["G"]:
                        pass
                    elif c == "S":
                        dma("S", "opS_0", sent_halves(0), ["DS_0"], "op0_7")
                    else:
                        swap(0, int(c), a, b, [o + "_0"] + (["send0"] if int(c) >= HOLD else []))
    done = ["D%d_0" % k for k in range(len(FIRST))]
    opps = [(span[str(k)][1], ["op%d_0" % k]) for k in range(len(FIRST))]

    span, at = {}, 0
    for name, n, mode in CHUNKS:
        span[name] = (at, at + n, mode)
        at += n
    bank_of, emptied = banks(ORDER["P"], 8)
    late = {}
    for t in range(1, STEPS):
        tag = "_%d" % t
        for q in "ADPG":
            for o in ORDER[q]:
                kind, c = o[0], o[1:]
                if o == "T":
                    send(t)
                    continue
                if c[0] == "S":
                    a, b = (0, S) if c == "S0" else (S, NS)
                    if kind == "G":
                        copy(q, o + tag, T.vs[:, a:b], W[t - 1][:, 0:A0].indirect(T.offs[:, a // 16:b // 16]),
                             done + ["opS_%d" % (t - 1), "offs"])
                    elif kind in "BA":
                        w, bank = (T.bendf if kind == "B" else T.mixf), bank_of[kind + "S"]
                        put(q, o + tag, [lambda a=a, b=b, w=w, bank=bank: P.matmul(ps[bank][:, a:b], w[:], T.vs[:, a:b], True, True)],
                            ["G" + c + tag, "bendf", "mixf"])
                    elif kind == "Q":
                        square(o + tag, T.sqs[:], bank_of["BS"], NS, ["BS0" + tag, "BS1" + tag])
                    else:
                        total(o + tag, T.hs[:, t * NS:(t + 1) * NS], bank_of["AS"], NS, T.sqs[:],
                              ["AS0" + tag, "AS1" + tag, "QS" + tag])
                    continue
                a, b, mode = span[c]
                n = b - a
                if q == "P":
                    side = "B" if kind in "hmB" else "A"
                    if mode == "f":
                        x, w, src = T.v, (T.bendf if side == "B" else T.mixf), "G"
                    else:
                        x, src = {"h": (T.hi, "H"), "i": (T.hi, "H"), "m": (T.mid, "M"), "n": (T.mid, "M")}.get(kind, (T.lo, "L"))
                        w = T.bendb if side == "B" else T.mixb
                        if mode == "z" and kind == "i":
                            src = "L"
                    out, opens, closes = ps[bank_of[side + c]][:, 0:n], o in emptied, kind in "BA"
                    put(q, o + tag, [lambda out=out, w=w, x=x[:, a:b], s=opens, e=closes: P.matmul(out, w[:], x, s, e)],
                        [src + c + tag] + ([emptied[o] + tag] if emptied.get(o) else []))
                elif kind in "GH":
                    src, deps = window(t - 1, a, b, done, opps)
                    copy(q, o + tag, (T.v if kind == "G" else T.hi)[:, a:b], src, deps)
                elif kind == "R":
                    src, deps = window(t - 1, a, b, done, opps)
                    put(q, o + tag, [lambda a=a, b=b, src=src: V.tensor_tensor(T.res[:, a:b], src, T.hi[:, a:b], Alu.subtract)],
                        deps + ["H" + c + tag])
                elif kind == "M":
                    copy(q, o + tag, T.mid[:, a:b], T.res[:, a:b], ["R" + c + tag])
                elif kind == "C":
                    copy(q, o + tag, ps[bank_of["A" + c]][:, 0:n], T.res[:, a:b],
                         ["R" + c + tag] + ([emptied["i" + c] + tag] if emptied["i" + c] else []))
                elif kind == "L":
                    src = ps[bank_of["A" + c]][:, 0:n] if mode == "z" else T.res[:, a:b]
                    put(q, o + tag, [lambda a=a, b=b, src=src: V.tensor_tensor(T.lo[:, a:b], src, T.mid[:, a:b], Alu.subtract)],
                        ["M" + c + tag] + (["C" + c + tag] if mode == "z" else []))
                elif kind == "Q":
                    square(o + tag, T.sq[:, a:b], bank_of["B" + c], n, ["B" + c + tag])
                else:
                    total(o + tag, W[t][:, H0 + a:H0 + b], bank_of["A" + c], n, T.sq[:, a:b], ["A" + c + tag, "Q" + c + tag])
        last = t == STEPS - 1
        opps = []
        for k, group in enumerate(SWAPS):
            if group == ["S"]:
                if not last:
                    dma("S", "opS" + tag, sent_halves(t), ["DS" + tag], "op%d_7" % t)
                continue
            a, b = span[group[0]][0], span[group[-1]][1]
            if last and group[0] in BY_ENGINE:
                for c in group:
                    late[c] = (span[c][0], span[c][1], ["D" + c + tag])
                    opps.append((span[c][1], ["X0" + c, "X1" + c]))
            else:
                swap(t, k, a, b, ["D" + c + tag for c in group])
                opps.append((b, ["op%d_%d" % (k, t)]))
        opps.sort()
        done = ["D" + x[0] + tag for x in CHUNKS]

    t = STEPS - 1
    for q in LAST:
        for kind, a, b in LAST[q]:
            if kind == "X":
                out, src = halves(t, *late[b][0:2])[a]
                copy(q, "X%d%s" % (a, b), out, src, late[b][2] + (["alone"] if q == "G" else []))
            else:
                src, deps = window(t, a, b, done, opps)
                copy(q, "F%d" % a, T.v[:, a:b], src, deps)
    for k, (a, b) in enumerate(STORES):
        dma("S", "st%d" % k, [(T.y[:, a:b], T.v[:, a:b])],
            ["F%d" % x[1] for q in LAST for x in LAST[q] if x[0] == "F" and a <= x[1] < b], "stored")

    token, count = dict(outside), {}
    for q in calls:
        for name, emit, deps, sem, inc in calls[q]:
            count[sem] = count.get(sem, 0) + inc * len(emit)
            token[name] = (sem, count[sem])
    for name in outside:
        count[outside[name][0]] = outside[name][1]
    clock = {name: (0, {outside[name][0]: outside[name][1]}) for name in outside}
    known = {q: {} for q in calls}
    waited = {}
    pos = {q: 0 for q in calls}
    serial = 0
    left = sum(len(calls[q]) for q in calls)
    while left:
        moved = False
        for q in calls:
            while pos[q] < len(calls[q]):
                name, emit, deps, sem, inc = calls[q][pos[q]]
                if any(d not in clock for d in deps if d != "alone"):
                    break
                if "alone" in deps:
                    deps = [d for d in deps if d != "alone"]
                    g.wait_ge(T.sem.cG, token[name][1] - len(emit))
                for d in sorted(set(deps), key=lambda d: (-clock[d][0], d)):
                    s, val = token[d]
                    if known[q].get(s, 0) < val:
                        queue[q].wait_ge(T.sem[s], val)
                        waited[s] = max(waited.get(s, 0), val)
                        for s2, v2 in clock[d][1].items():
                            known[q][s2] = max(known[q].get(s2, 0), v2)
                for e in emit:
                    ins = e()
                    if ins is not None:
                        ins.then_inc(T.sem[sem], inc)
                serial += 1
                seen = dict(known[q])
                seen[sem] = token[name][1]
                clock[name] = (serial, seen)
                pos[q] += 1
                left -= 1
                moved = True
        assert moved
    for s in sorted(count, key=lambda s: s == "stored"):
        if waited.get(s, 0) < count[s]:
            g.wait_ge(T.sem[s], count[s])
